import numpy as np
import ml_dtypes


def mxq(x, axis, fmt="e4m3"):
    dtype, down = {"e4m3": (ml_dtypes.float8_e4m3fn, 7), "e5m2": (ml_dtypes.float8_e5m2, 14)}[fmt]
    v = np.moveaxis(np.asarray(x, np.float32).astype(ml_dtypes.bfloat16).astype(np.float64), axis, -1)
    blocks = v.reshape(v.shape[:-1] + (-1, 32))
    amax = np.abs(blocks).max(-1, keepdims=True)
    byte = np.maximum(np.where(amax > 0, np.frexp(amax)[1] - 1 + 127, 0) - down, 1)
    scale = np.exp2(byte - 127.0)
    codes = (blocks / scale).astype(np.float32).astype(dtype).astype(np.float64)
    return np.moveaxis((codes * scale).reshape(v.shape), -1, axis)


WIDE = False


def mx_kscale(k):
    if not WIDE:
        return np.ones(k)
    levels = np.array([10, -10, 5, -5, 0])
    if k % 512:
        return np.exp2(np.random.permutation(np.resize(levels, k // 32))).repeat(32)
    a = np.empty((k // 512, 16))
    for p in range(k // 512):
        a[p, :8] = np.random.permutation(np.resize(levels, 8))
        for g in range(8):
            far = levels[np.abs(levels - a[p, g]) >= 10]
            a[p, g + 8] = far[np.random.randint(len(far))]
    return np.exp2(a.ravel()).repeat(32)


def f64(x):
    return np.asarray(x).astype(np.float64)


def striped(idx):
    return np.tile(idx.reshape(-1, 16).T, (8, 1)).astype(np.uint16)


def unstriped(offs):
    return offs[:16].T.reshape(-1).astype(np.int64)


def pack_weight(w):
    k, n = w.shape
    w = f64(np.asarray(w, np.float32).astype(ml_dtypes.bfloat16)).reshape(k // 32, 32, n)
    amax = np.abs(w).max(1)
    byte = np.clip(np.where(amax > 0, np.frexp(amax)[1] - 1 + 127 - 7, 1), 1, 254)
    scaled = (w * np.exp2(127.0 - byte)[:, None, :]).reshape(k, n).astype(np.float32)
    words = np.ascontiguousarray(scaled.reshape(k // 512, 128, 4, n).transpose(0, 1, 3, 2)).astype(ml_dtypes.float8_e4m3fn).view(np.uint8)
    return words, np.ascontiguousarray(byte.astype(np.uint8).reshape(k // 512, 16, n))


def unpack_weight(words, scales):
    g, p, n, _ = words.shape
    vals = np.ascontiguousarray(words).view(ml_dtypes.float8_e4m3fn).astype(np.float64) * np.repeat(np.exp2(scales.astype(np.float64) - 127.0), 8, axis=1)[..., None]
    return vals.transpose(0, 1, 3, 2).reshape(g * 512, n)


def silu(v):
    return v / (1.0 + np.exp(-np.maximum(v, -700.0)))


K, T, S, N, U = 1024, 2048, 512, 256, 1024


def setup_inputs():
    n = np.random.standard_normal
    s = mx_kscale(K)[:, None]
    packed_w1 = pack_weight(n((K, N)) / np.sqrt(K) / s)
    return {
        "xT": (n((K, T)) * s).astype(np.float32),
        "w1_words": packed_w1[0],
        "w1_scales": packed_w1[1],
        "gamma": np.random.uniform(0.5, 1.5, (N, U)).astype(np.float32),
        "beta": (0.5 * n((N, U))).astype(np.float32),
        "offs": striped(np.random.permutation(T)[:S]),
        "cls": striped(np.random.randint(0, U, S)),
    }


def reference(xT, w1_words, w1_scales, gamma, beta, offs, cls):
    xq = mxq(f64(xT)[:, unstriped(offs)], 0, "e4m3")
    y = unpack_weight(w1_words, w1_scales).T @ xq
    g = f64(gamma)[:, unstriped(cls)]
    s = f64(beta)[:, unstriped(cls)]
    return silu(y * g + s)

@@ -1,0 +1,130 @@
+from contextlib import ExitStack
+
+import concourse.mybir as mybir
+
+K, T, S, N, U = 1024, 2048, 512, 256, 1024
+FLOPS = 2 * K * N * S
+
+F32 = mybir.dt.float32
+BF16 = mybir.dt.bfloat16
+I32 = mybir.dt.int32
+U32 = mybir.dt.uint32
+U16 = mybir.dt.uint16
+U8 = mybir.dt.uint8
+FP8X4 = mybir.dt.float8_e4m3fn_x4
+MULT = mybir.AluOpType.mult
+ADD = mybir.AluOpType.add
+SILU = mybir.ActivationFunctionType.Silu
+
+P = 128
+PACK = 4
+PASSES = K // (P * PACK)
+HALF = S // 2
+LIST_COLS = S // 16
+
+
+def tile_picked_cbn_silu_e_kernel(tc, xT, w1_words, w1_scales, gamma, beta, offs, cls, out):
+    nc = tc.nc
+    with ExitStack() as ctx:
+        keep = ctx.enter_context(tc.tile_pool(name="keep", bufs=1))
+        psum = ctx.enter_context(tc.psum_pool(name="psum", bufs=1))
+
+        offs_sb = keep.tile([P, LIST_COLS], U16, name="offs_sb")
+        cls_sb = keep.tile([P, LIST_COLS], U16, name="cls_sb")
+        pairs = [keep.tile([P, 2, T], F32, name=f"xp{u}") for u in range(2)]
+        singles = [keep.tile([P, T], F32, name=f"xs{j}") for j in range(PACK)]
+        planes = [[pairs[j // 2][:, j % 2, :] for j in range(PACK)], [singles[j][:] for j in range(PACK)]]
+        w_codes = [keep.tile([P, N], U32, name=f"w_codes{z}", align_bytes=64) for z in range(PASSES)]
+        w_scale = keep.tile([P, N], U8, name="w_scale", align_bytes=64)
+        gam = [keep.tile([P, U], F32, name=f"gam{b}") for b in range(2)]
+        bet = [keep.tile([P, U], F32, name=f"bet{b}") for b in range(2)]
+        warm = keep.tile([P, 8], F32, name="warm")
+        warm_out = keep.tile([P, 8], F32, name="warm_out")
+
+        x_rows = xT.rearrange("(z p j) t -> z p j t", z=PASSES, j=PACK)
+
+        nc.vector.memset(warm[:], 0.0)
+        nc.scalar.activation(warm_out[:], warm[:], SILU)
+
+        nc.gpsimd.memset(w_scale[:].bitcast(I32), 0)
+        scales_i32 = w1_scales.bitcast(I32)
+        for q in range(4):
+            nc.gpsimd.dma_start(w_scale[:].bitcast(I32)[32 * q : 32 * q + 4 * PASSES, :], scales_i32[:, 4 * q : 4 * q + 4, :])
+
+        nc.sync.dma_start(pairs[0][:], x_rows[0, :, 0:2, :])
+        nc.sync.dma_start(offs_sb[:], offs)
+        nc.sync.dma_start(pairs[1][:], x_rows[0, :, 2:4, :])
+        for j in range(PACK):
+            nc.sync.dma_start(singles[j][:], x_rows[1, :, j, :])
+        for z in range(PASSES):
+            nc.sync.dma_start(w_codes[z][:].bitcast(I32), w1_words[z].rearrange("p n r -> p (n r)").bitcast(I32))
+        nc.sync.dma_start(cls_sb[:], cls)
+        nc.sync.dma_start(gam[0][:], gamma[0:P, :])
+        nc.sync.dma_start(gam[1][:], gamma[P : 2 * P, :])
+        nc.sync.dma_start(bet[0][:], beta[0:P, :])
+        nc.sync.dma_start(bet[1][:], beta[P : 2 * P, :])
+
+        picked = [keep.tile([P, S, PACK], BF16, name=f"picked{z}", align_bytes=64) for z in range(PASSES)]
+        codes = [keep.tile([P, S], U32, name=f"codes{z}", align_bytes=64) for z in range(PASSES)]
+        scale = [keep.tile([P, S], U8, name=f"scale{z}", align_bytes=64) for z in range(PASSES)]
+        acc = [[psum.tile([P, HALF], F32, name=f"acc{b}{h}") for h in range(2)] for b in range(2)]
+
+        def cols(h):
+            return slice(h * HALF, (h + 1) * HALF)
+
+        def list_cols(h):
+            return slice(h * LIST_COLS // 2, (h + 1) * LIST_COLS // 2)
+
+        def quantize(z, lo, hi):
+            nc.vector.quantize_mx(
+                out=codes[z][:, lo:hi].bitcast(FP8X4),
+                scales=scale[z][:, lo:hi],
+                in_=picked[z][:, lo:hi, :].rearrange("p s j -> p (s j)"),
+            )
+
+        def multiply(z, h):
+            for b in range(2):
+                nc.tensor.matmul_mx(
+                    out=acc[b][h][:],
+                    lhsT=w_codes[z][:, b * P : (b + 1) * P].bitcast(FP8X4),
+                    lhsT_scale=w_scale[4 * z :, b * P : (b + 1) * P],
+                    rhs=codes[z][:, cols(h)].bitcast(FP8X4),
+                    rhs_scale=scale[z][:, cols(h)],
+                    start=(z == 0),
+                    stop=(z == PASSES - 1),
+                )
+
+        for j in range(PACK):
+            nc.vector.tensor_copy(picked[0][:, :, j], planes[0][j].indirect(offs_sb[:]))
+        quantize(0, 0, S)
+        for h in range(2):
+            multiply(0, h)
+        for j in range(PACK - 1):
+            nc.vector.tensor_copy(picked[1][:, :, j], planes[1][j].indirect(offs_sb[:]))
+        for h in range(2):
+            nc.vector.tensor_copy(picked[1][:, cols(h), PACK - 1], planes[1][PACK - 1].indirect(offs_sb[:, list_cols(h)]))
+        for h in range(2):
+            quantize(1, h * HALF, (h + 1) * HALF)
+            multiply(1, h)
+
+        g0 = keep.tile([P, HALF], F32, name="g0")
+        y0 = keep.tile([P, HALF], F32, name="y0")
+        y1 = keep.tile([P, S], F32, name="y1")
+        yg = [keep.tile([P, S], F32, name=f"yg{b}") for b in range(2)]
+        u = [keep.tile([P, S], F32, name=f"u{b}") for b in range(2)]
+        res = [keep.tile([P, S], F32, name=f"res{b}") for b in range(2)]
+
+        nc.scalar.copy(y0[:], acc[0][0][:])
+        for h in range(2):
+            nc.scalar.copy(y1[:, cols(h)], acc[1][h][:])
+        nc.vector.tensor_copy(g0[:], gam[0][:].indirect(cls_sb[:, list_cols(1)]))
+        nc.vector.tensor_tensor(yg[0][:, cols(0)], gam[0][:].indirect(cls_sb[:, list_cols(0)]), y0[:], MULT)
+        nc.vector.tensor_tensor(yg[0][:, cols(1)], acc[0][1][:], g0[:], MULT)
+        nc.vector.tensor_tensor(yg[1][:], gam[1][:].indirect(cls_sb[:]), y1[:], MULT)
+        nc.vector.tensor_tensor(u[0][:], bet[0][:].indirect(cls_sb[:]), yg[0][:], ADD)
+        nc.scalar.activation(res[0][:], u[0][:], SILU)
+        nc.sync.dma_start(out[0:P, :], res[0][:])
+        for lo, hi in ((0, 256), (256, 384), (384, 512)):
+            nc.vector.tensor_tensor(u[1][:, lo:hi], bet[1][:].indirect(cls_sb[:, lo // 16 : hi // 16]), yg[1][:, lo:hi], ADD)
+            nc.scalar.activation(res[1][:, lo:hi], u[1][:, lo:hi], SILU)
+            nc.sync.dma_start(out[P : 2 * P, lo:hi], res[1][:, lo:hi])

@@ -31,9 +31,8 @@ def tile_picked_cbn_silu_e_kernel(tc, xT, w1_words, w1_scales, gamma, beta, offs
 
         offs_sb = keep.tile([P, LIST_COLS], U16, name="offs_sb")
         cls_sb = keep.tile([P, LIST_COLS], U16, name="cls_sb")
-        pairs = [keep.tile([P, 2, T], F32, name=f"xp{u}") for u in range(2)]
-        singles = [keep.tile([P, T], F32, name=f"xs{j}") for j in range(PACK)]
-        planes = [[pairs[j // 2][:, j % 2, :] for j in range(PACK)], [singles[j][:] for j in range(PACK)]]
+        plane_tiles = [[keep.tile([P, T], F32, name=f"x{z}{j}") for j in range(PACK)] for z in range(PASSES)]
+        planes = [[plane_tiles[z][j][:] for j in range(PACK)] for z in range(PASSES)]
         w_codes = [keep.tile([P, N], U32, name=f"w_codes{z}", align_bytes=64) for z in range(PASSES)]
         w_scale = keep.tile([P, N], U8, name="w_scale", align_bytes=64)
         gam = [keep.tile([P, U], F32, name=f"gam{b}") for b in range(2)]
@@ -51,11 +50,11 @@ def tile_picked_cbn_silu_e_kernel(tc, xT, w1_words, w1_scales, gamma, beta, offs
         for q in range(4):
             nc.gpsimd.dma_start(w_scale[:].bitcast(I32)[32 * q : 32 * q + 4 * PASSES, :], scales_i32[:, 4 * q : 4 * q + 4, :])
 
-        nc.sync.dma_start(pairs[0][:], x_rows[0, :, 0:2, :])
-        nc.sync.dma_start(offs_sb[:], offs)
-        nc.sync.dma_start(pairs[1][:], x_rows[0, :, 2:4, :])
-        for j in range(PACK):
-            nc.sync.dma_start(singles[j][:], x_rows[1, :, j, :])
+        for z in range(PASSES):
+            for j in range(PACK):
+                nc.sync.dma_start(planes[z][j], x_rows[z, :, j, :])
+                if (z, j) == (0, 0):
+                    nc.sync.dma_start(offs_sb[:], offs)
         for z in range(PASSES):
             nc.sync.dma_start(w_codes[z][:].bitcast(I32), w1_words[z].rearrange("p n r -> p (n r)").bitcast(I32))
         nc.sync.dma_start(cls_sb[:], cls)

@@ -20,6 +20,10 @@ P = 128
 PACK = 4
 PASSES = K // (P * PACK)
 HALF = S // 2
+LAST = 3
+ORDER = ((0, 1, 2, 3), (2, 0, 1, 3))
+CHUNKS = ((0, 512), (512, 1024), (1024, 1536), (1536, 2048))
+COPY = mybir.ActivationFunctionType.Copy
 LIST_COLS = S // 16
 
 
@@ -51,8 +55,12 @@ def tile_picked_cbn_silu_e_kernel(tc, xT, w1_words, w1_scales, gamma, beta, offs
             nc.gpsimd.dma_start(w_scale[:].bitcast(I32)[32 * q : 32 * q + 4 * PASSES, :], scales_i32[:, 4 * q : 4 * q + 4, :])
 
         for z in range(PASSES):
-            for j in range(PACK):
-                nc.sync.dma_start(planes[z][j], x_rows[z, :, j, :])
+            for j in ORDER[z]:
+                if (z, j) == (PASSES - 1, LAST):
+                    for lo, hi in CHUNKS:
+                        nc.sync.dma_start(plane_tiles[z][j][:, lo:hi], x_rows[z, :, j, lo:hi])
+                else:
+                    nc.sync.dma_start(planes[z][j], x_rows[z, :, j, :])
                 if (z, j) == (0, 0):
                     nc.sync.dma_start(offs_sb[:], offs)
         for z in range(PASSES):
@@ -98,32 +106,41 @@ def tile_picked_cbn_silu_e_kernel(tc, xT, w1_words, w1_scales, gamma, beta, offs
         quantize(0, 0, S)
         for h in range(2):
             multiply(0, h)
-        for j in range(PACK - 1):
+        flat = keep.tile([P, HALF], BF16, name="flat")
+        rounded = keep.tile([P, T], BF16, name="rounded")
+        nc.vector.tensor_copy(picked[1][:, cols(0), 2], planes[1][2].indirect(offs_sb[:, list_cols(0)]))
+        nc.vector.tensor_copy(flat[:], planes[1][2].indirect(offs_sb[:, list_cols(1)]))
+        nc.scalar.copy(picked[1][:, cols(1), 2], flat[:])
+        for j in range(2):
             nc.vector.tensor_copy(picked[1][:, :, j], planes[1][j].indirect(offs_sb[:]))
-        for h in range(2):
-            nc.vector.tensor_copy(picked[1][:, cols(h), PACK - 1], planes[1][PACK - 1].indirect(offs_sb[:, list_cols(h)]))
+        for lo, hi in CHUNKS:
+            nc.scalar.copy(rounded[:, lo:hi], plane_tiles[1][LAST][:, lo:hi])
+        nc.vector.tensor_copy(picked[1][:, cols(0), LAST], planes[1][LAST].indirect(offs_sb[:, list_cols(0)]))
+        nc.scalar.activation(picked[1][:, cols(1), LAST], rounded[:].indirect(offs_sb[:, list_cols(1)]), COPY)
         for h in range(2):
             quantize(1, h * HALF, (h + 1) * HALF)
             multiply(1, h)
 
-        g0 = keep.tile([P, HALF], F32, name="g0")
-        y0 = keep.tile([P, HALF], F32, name="y0")
-        y1 = keep.tile([P, S], F32, name="y1")
+        y = [keep.tile([P, S], F32, name=f"y{b}") for b in range(2)]
         yg = [keep.tile([P, S], F32, name=f"yg{b}") for b in range(2)]
         u = [keep.tile([P, S], F32, name=f"u{b}") for b in range(2)]
         res = [keep.tile([P, S], F32, name=f"res{b}") for b in range(2)]
 
-        nc.scalar.copy(y0[:], acc[0][0][:])
-        for h in range(2):
-            nc.scalar.copy(y1[:, cols(h)], acc[1][h][:])
+        g0 = keep.tile([P, HALF], F32, name="g0")
         nc.vector.tensor_copy(g0[:], gam[0][:].indirect(cls_sb[:, list_cols(1)]))
-        nc.vector.tensor_tensor(yg[0][:, cols(0)], gam[0][:].indirect(cls_sb[:, list_cols(0)]), y0[:], MULT)
-        nc.vector.tensor_tensor(yg[0][:, cols(1)], acc[0][1][:], g0[:], MULT)
-        nc.vector.tensor_tensor(yg[1][:], gam[1][:].indirect(cls_sb[:]), y1[:], MULT)
-        nc.vector.tensor_tensor(u[0][:], bet[0][:].indirect(cls_sb[:]), yg[0][:], ADD)
-        nc.scalar.activation(res[0][:], u[0][:], SILU)
-        nc.sync.dma_start(out[0:P, :], res[0][:])
+        for h in range(2):
+            for b in range(2):
+                if (b, h) == (0, 1):
+                    nc.vector.tensor_tensor(yg[b][:, cols(h)], acc[b][h][:], g0[:], MULT)
+                else:
+                    nc.scalar.copy(y[b][:, cols(h)], acc[b][h][:])
+                    nc.vector.tensor_tensor(yg[b][:, cols(h)], gam[b][:].indirect(cls_sb[:, list_cols(h)]), y[b][:, cols(h)], MULT)
+
+        def shift_and_store(b, lo, hi):
+            nc.vector.tensor_tensor(u[b][:, lo:hi], bet[b][:].indirect(cls_sb[:, lo // 16 : hi // 16]), yg[b][:, lo:hi], ADD)
+            nc.scalar.activation(res[b][:, lo:hi], u[b][:, lo:hi], SILU)
+            nc.sync.dma_start(out[b * P : (b + 1) * P, lo:hi], res[b][:, lo:hi])
+
+        shift_and_store(0, 0, S)
         for lo, hi in ((0, 256), (256, 384), (384, 512)):
-            nc.vector.tensor_tensor(u[1][:, lo:hi], bet[1][:].indirect(cls_sb[:, lo // 16 : hi // 16]), yg[1][:, lo:hi], ADD)
-            nc.scalar.activation(res[1][:, lo:hi], u[1][:, lo:hi], SILU)
-            nc.sync.dma_start(out[P : 2 * P, lo:hi], res[1][:, lo:hi])
+            shift_and_store(1, lo, hi)

@@ -22,7 +22,7 @@ PASSES = K // (P * PACK)
 HALF = S // 2
 LAST = 3
 ORDER = ((0, 1, 2, 3), (2, 0, 1, 3))
-CHUNKS = ((0, 512), (512, 1024), (1024, 1536), (1536, 2048))
+CHUNKS = ((0, 640), (640, 1280), (1280, 1792), (1792, 2048))
 COPY = mybir.ActivationFunctionType.Copy
 LIST_COLS = S // 16
 
@@ -41,13 +41,8 @@ def tile_picked_cbn_silu_e_kernel(tc, xT, w1_words, w1_scales, gamma, beta, offs
         w_scale = keep.tile([P, N], U8, name="w_scale", align_bytes=64)
         gam = [keep.tile([P, U], F32, name=f"gam{b}") for b in range(2)]
         bet = [keep.tile([P, U], F32, name=f"bet{b}") for b in range(2)]
-        warm = keep.tile([P, 8], F32, name="warm")
-        warm_out = keep.tile([P, 8], F32, name="warm_out")
 
         x_rows = xT.rearrange("(z p j) t -> z p j t", z=PASSES, j=PACK)
-
-        nc.vector.memset(warm[:], 0.0)
-        nc.scalar.activation(warm_out[:], warm[:], SILU)
 
         nc.gpsimd.memset(w_scale[:].bitcast(I32), 0)
         scales_i32 = w1_scales.bitcast(I32)
@@ -113,8 +108,11 @@ def tile_picked_cbn_silu_e_kernel(tc, xT, w1_words, w1_scales, gamma, beta, offs
         nc.scalar.copy(picked[1][:, cols(1), 2], flat[:])
         for j in range(2):
             nc.vector.tensor_copy(picked[1][:, :, j], planes[1][j].indirect(offs_sb[:]))
-        for lo, hi in CHUNKS:
-            nc.scalar.copy(rounded[:, lo:hi], plane_tiles[1][LAST][:, lo:hi])
+        for c, (lo, hi) in enumerate(CHUNKS):
+            if c == 2:
+                nc.vector.tensor_copy(rounded[:, lo:hi], plane_tiles[1][LAST][:, lo:hi])
+            else:
+                nc.scalar.copy(rounded[:, lo:hi], plane_tiles[1][LAST][:, lo:hi])
         nc.vector.tensor_copy(picked[1][:, cols(0), LAST], planes[1][LAST].indirect(offs_sb[:, list_cols(0)]))
         nc.scalar.activation(picked[1][:, cols(1), LAST], rounded[:].indirect(offs_sb[:, list_cols(1)]), COPY)
         for h in range(2):

@@ -21,8 +21,8 @@ PACK = 4
 PASSES = K // (P * PACK)
 HALF = S // 2
 LAST = 3
-ORDER = ((0, 1, 2, 3), (2, 0, 1, 3))
-CHUNKS = ((0, 640), (640, 1280), (1280, 1792), (1792, 2048))
+ORDER = (2, 0, 1)
+CHUNKS = ((0, 1024), (1024, 1696), (1696, 2048))
 COPY = mybir.ActivationFunctionType.Copy
 LIST_COLS = S // 16
 
@@ -35,8 +35,9 @@ def tile_picked_cbn_silu_e_kernel(tc, xT, w1_words, w1_scales, gamma, beta, offs
 
         offs_sb = keep.tile([P, LIST_COLS], U16, name="offs_sb")
         cls_sb = keep.tile([P, LIST_COLS], U16, name="cls_sb")
-        plane_tiles = [[keep.tile([P, T], F32, name=f"x{z}{j}") for j in range(PACK)] for z in range(PASSES)]
-        planes = [[plane_tiles[z][j][:] for j in range(PACK)] for z in range(PASSES)]
+        pairs = [keep.tile([P, 2, T], F32, name=f"pair{u}") for u in range(2)]
+        singles = [keep.tile([P, T], F32, name=f"x1{j}") for j in range(PACK)]
+        planes = [[pairs[j // 2][:, j % 2, :] for j in range(PACK)], [singles[j][:] for j in range(PACK)]]
         w_codes = [keep.tile([P, N], U32, name=f"w_codes{z}", align_bytes=64) for z in range(PASSES)]
         w_scale = keep.tile([P, N], U8, name="w_scale", align_bytes=64)
         gam = [keep.tile([P, U], F32, name=f"gam{b}") for b in range(2)]
@@ -49,15 +50,14 @@ def tile_picked_cbn_silu_e_kernel(tc, xT, w1_words, w1_scales, gamma, beta, offs
         for q in range(4):
             nc.gpsimd.dma_start(w_scale[:].bitcast(I32)[32 * q : 32 * q + 4 * PASSES, :], scales_i32[:, 4 * q : 4 * q + 4, :])
 
-        for z in range(PASSES):
-            for j in ORDER[z]:
-                if (z, j) == (PASSES - 1, LAST):
-                    for lo, hi in CHUNKS:
-                        nc.sync.dma_start(plane_tiles[z][j][:, lo:hi], x_rows[z, :, j, lo:hi])
-                else:
-                    nc.sync.dma_start(planes[z][j], x_rows[z, :, j, :])
-                if (z, j) == (0, 0):
-                    nc.sync.dma_start(offs_sb[:], offs)
+        for u in range(2):
+            nc.sync.dma_start(pairs[u][:], x_rows[0, :, 2 * u : 2 * u + 2, :])
+            if u == 0:
+                nc.sync.dma_start(offs_sb[:], offs)
+        for j in ORDER:
+            nc.sync.dma_start(planes[1][j], x_rows[1, :, j, :])
+        for lo, hi in CHUNKS:
+            nc.sync.dma_start(singles[LAST][:, lo:hi], x_rows[1, :, LAST, lo:hi])
         for z in range(PASSES):
             nc.sync.dma_start(w_codes[z][:].bitcast(I32), w1_words[z].rearrange("p n r -> p (n r)").bitcast(I32))
         nc.sync.dma_start(cls_sb[:], cls)
@@ -96,8 +96,13 @@ def tile_picked_cbn_silu_e_kernel(tc, xT, w1_words, w1_scales, gamma, beta, offs
                     stop=(z == PASSES - 1),
                 )
 
+        gathered = keep.tile([P, PACK, S], F32, name="gathered")
         for j in range(PACK):
-            nc.vector.tensor_copy(picked[0][:, :, j], planes[0][j].indirect(offs_sb[:]))
+            nc.vector.tensor_copy(gathered[:, j, :], planes[0][j].indirect(offs_sb[:]))
+        nc.scalar.copy(
+            picked[0][:].rearrange("p (c i) j -> p c j i", i=4),
+            gathered[:].rearrange("p j (c i) -> p c j i", i=4),
+        )
         quantize(0, 0, S)
         for h in range(2):
             multiply(0, h)
@@ -109,10 +114,10 @@ def tile_picked_cbn_silu_e_kernel(tc, xT, w1_words, w1_scales, gamma, beta, offs
         for j in range(2):
             nc.vector.tensor_copy(picked[1][:, :, j], planes[1][j].indirect(offs_sb[:]))
         for c, (lo, hi) in enumerate(CHUNKS):
-            if c == 2:
-                nc.vector.tensor_copy(rounded[:, lo:hi], plane_tiles[1][LAST][:, lo:hi])
+            if c == 1:
+                nc.vector.tensor_copy(rounded[:, lo:hi], singles[LAST][:, lo:hi])
             else:
-                nc.scalar.copy(rounded[:, lo:hi], plane_tiles[1][LAST][:, lo:hi])
+                nc.scalar.copy(rounded[:, lo:hi], singles[LAST][:, lo:hi])
         nc.vector.tensor_copy(picked[1][:, cols(0), LAST], planes[1][LAST].indirect(offs_sb[:, list_cols(0)]))
         nc.scalar.activation(picked[1][:, cols(1), LAST], rounded[:].indirect(offs_sb[:, list_cols(1)]), COPY)
         for h in range(2):
@@ -139,6 +144,7 @@ def tile_picked_cbn_silu_e_kernel(tc, xT, w1_words, w1_scales, gamma, beta, offs
             nc.scalar.activation(res[b][:, lo:hi], u[b][:, lo:hi], SILU)
             nc.sync.dma_start(out[b * P : (b + 1) * P, lo:hi], res[b][:, lo:hi])
 
-        shift_and_store(0, 0, S)
+        for h in range(2):
+            shift_and_store(0, h * HALF, (h + 1) * HALF)
         for lo, hi in ((0, 256), (256, 384), (384, 512)):
             shift_and_store(1, lo, hi)

@@ -1,6 +1,7 @@
 from contextlib import ExitStack
 
 import concourse.mybir as mybir
+from concourse.masks import make_identity
 
 K, T, S, N, U = 1024, 2048, 512, 256, 1024
 FLOPS = 2 * K * N * S
@@ -21,8 +22,8 @@ PACK = 4
 PASSES = K // (P * PACK)
 HALF = S // 2
 LAST = 3
-ORDER = (2, 0, 1)
-CHUNKS = ((0, 1024), (1024, 1696), (1696, 2048))
+ORDER = ((0, 1, 2, 3), (2, 0, 1, 3))
+CHUNKS = ((0, 640), (640, 1280), (1280, 1792), (1792, 2048))
 COPY = mybir.ActivationFunctionType.Copy
 LIST_COLS = S // 16
 
@@ -35,13 +36,15 @@ def tile_picked_cbn_silu_e_kernel(tc, xT, w1_words, w1_scales, gamma, beta, offs
 
         offs_sb = keep.tile([P, LIST_COLS], U16, name="offs_sb")
         cls_sb = keep.tile([P, LIST_COLS], U16, name="cls_sb")
-        pairs = [keep.tile([P, 2, T], F32, name=f"pair{u}") for u in range(2)]
-        singles = [keep.tile([P, T], F32, name=f"x1{j}") for j in range(PACK)]
-        planes = [[pairs[j // 2][:, j % 2, :] for j in range(PACK)], [singles[j][:] for j in range(PACK)]]
+        plane_tiles = [[keep.tile([P, T], F32, name=f"x{z}{j}") for j in range(PACK)] for z in range(PASSES)]
+        planes = [[plane_tiles[z][j][:] for j in range(PACK)] for z in range(PASSES)]
         w_codes = [keep.tile([P, N], U32, name=f"w_codes{z}", align_bytes=64) for z in range(PASSES)]
         w_scale = keep.tile([P, N], U8, name="w_scale", align_bytes=64)
         gam = [keep.tile([P, U], F32, name=f"gam{b}") for b in range(2)]
         bet = [keep.tile([P, U], F32, name=f"bet{b}") for b in range(2)]
+
+        ident = keep.tile([P, P], F32, name="ident")
+        make_identity(nc, ident[:])
 
         x_rows = xT.rearrange("(z p j) t -> z p j t", z=PASSES, j=PACK)
 
@@ -50,20 +53,21 @@ def tile_picked_cbn_silu_e_kernel(tc, xT, w1_words, w1_scales, gamma, beta, offs
         for q in range(4):
             nc.gpsimd.dma_start(w_scale[:].bitcast(I32)[32 * q : 32 * q + 4 * PASSES, :], scales_i32[:, 4 * q : 4 * q + 4, :])
 
-        for u in range(2):
-            nc.sync.dma_start(pairs[u][:], x_rows[0, :, 2 * u : 2 * u + 2, :])
-            if u == 0:
-                nc.sync.dma_start(offs_sb[:], offs)
-        for j in ORDER:
-            nc.sync.dma_start(planes[1][j], x_rows[1, :, j, :])
-        for lo, hi in CHUNKS:
-            nc.sync.dma_start(singles[LAST][:, lo:hi], x_rows[1, :, LAST, lo:hi])
+        for z in range(PASSES):
+            for j in ORDER[z]:
+                if (z, j) == (PASSES - 1, LAST):
+                    for lo, hi in CHUNKS:
+                        nc.sync.dma_start(plane_tiles[z][j][:, lo:hi], x_rows[z, :, j, lo:hi])
+                else:
+                    nc.sync.dma_start(planes[z][j], x_rows[z, :, j, :])
+                if (z, j) == (0, 0):
+                    nc.sync.dma_start(offs_sb[:], offs)
         for z in range(PASSES):
             nc.sync.dma_start(w_codes[z][:].bitcast(I32), w1_words[z].rearrange("p n r -> p (n r)").bitcast(I32))
         nc.sync.dma_start(cls_sb[:], cls)
+        nc.sync.dma_start(bet[0][:], beta[0:P, :])
         nc.sync.dma_start(gam[0][:], gamma[0:P, :])
         nc.sync.dma_start(gam[1][:], gamma[P : 2 * P, :])
-        nc.sync.dma_start(bet[0][:], beta[0:P, :])
         nc.sync.dma_start(bet[1][:], beta[P : 2 * P, :])
 
         picked = [keep.tile([P, S, PACK], BF16, name=f"picked{z}", align_bytes=64) for z in range(PASSES)]
@@ -84,8 +88,8 @@ def tile_picked_cbn_silu_e_kernel(tc, xT, w1_words, w1_scales, gamma, beta, offs
                 in_=picked[z][:, lo:hi, :].rearrange("p s j -> p (s j)"),
             )
 
-        def multiply(z, h):
-            for b in range(2):
+        def multiply(z, b, h):
+            if True:
                 nc.tensor.matmul_mx(
                     out=acc[b][h][:],
                     lhsT=w_codes[z][:, b * P : (b + 1) * P].bitcast(FP8X4),
@@ -96,16 +100,12 @@ def tile_picked_cbn_silu_e_kernel(tc, xT, w1_words, w1_scales, gamma, beta, offs
                     stop=(z == PASSES - 1),
                 )
 
-        gathered = keep.tile([P, PACK, S], F32, name="gathered")
         for j in range(PACK):
-            nc.vector.tensor_copy(gathered[:, j, :], planes[0][j].indirect(offs_sb[:]))
-        nc.scalar.copy(
-            picked[0][:].rearrange("p (c i) j -> p c j i", i=4),
-            gathered[:].rearrange("p j (c i) -> p c j i", i=4),
-        )
+            nc.vector.tensor_copy(picked[0][:, :, j], planes[0][j].indirect(offs_sb[:]))
         quantize(0, 0, S)
-        for h in range(2):
-            multiply(0, h)
+        for b in range(2):
+            for h in range(2):
+                multiply(0, b, h)
         flat = keep.tile([P, HALF], BF16, name="flat")
         rounded = keep.tile([P, T], BF16, name="rounded")
         nc.vector.tensor_copy(picked[1][:, cols(0), 2], planes[1][2].indirect(offs_sb[:, list_cols(0)]))
@@ -114,37 +114,47 @@ def tile_picked_cbn_silu_e_kernel(tc, xT, w1_words, w1_scales, gamma, beta, offs
         for j in range(2):
             nc.vector.tensor_copy(picked[1][:, :, j], planes[1][j].indirect(offs_sb[:]))
         for c, (lo, hi) in enumerate(CHUNKS):
-            if c == 1:
-                nc.vector.tensor_copy(rounded[:, lo:hi], singles[LAST][:, lo:hi])
+            if c == 2:
+                nc.vector.tensor_copy(rounded[:, lo:hi], plane_tiles[1][LAST][:, lo:hi])
             else:
-                nc.scalar.copy(rounded[:, lo:hi], singles[LAST][:, lo:hi])
+                nc.scalar.copy(rounded[:, lo:hi], plane_tiles[1][LAST][:, lo:hi])
         nc.vector.tensor_copy(picked[1][:, cols(0), LAST], planes[1][LAST].indirect(offs_sb[:, list_cols(0)]))
         nc.scalar.activation(picked[1][:, cols(1), LAST], rounded[:].indirect(offs_sb[:, list_cols(1)]), COPY)
         for h in range(2):
             quantize(1, h * HALF, (h + 1) * HALF)
-            multiply(1, h)
+        for b in range(2):
+            for h in range(2):
+                multiply(1, b, h)
 
         y = [keep.tile([P, S], F32, name=f"y{b}") for b in range(2)]
         yg = [keep.tile([P, S], F32, name=f"yg{b}") for b in range(2)]
-        u = [keep.tile([P, S], F32, name=f"u{b}") for b in range(2)]
+        u1 = keep.tile([P, S], F32, name="u1")
         res = [keep.tile([P, S], F32, name=f"res{b}") for b in range(2)]
+        b0 = keep.tile([P, S], F32, name="b0")
+        turned = keep.tile([P, S], F32, name="turned")
+        sums = [psum.tile([P, HALF], F32, name=f"sums{h}") for h in range(2)]
+        back = [psum.tile([P, HALF], F32, name=f"back{h}") for h in range(2)]
 
-        g0 = keep.tile([P, HALF], F32, name="g0")
-        nc.vector.tensor_copy(g0[:], gam[0][:].indirect(cls_sb[:, list_cols(1)]))
+        nc.vector.tensor_copy(b0[:], bet[0][:].indirect(cls_sb[:]))
+        for b in range(2):
+            for h in range(2):
+                nc.scalar.copy(y[b][:, cols(h)], acc[b][h][:])
+        for b in range(2):
+            for h in range(2):
+                nc.vector.tensor_tensor(yg[b][:, cols(h)], gam[b][:].indirect(cls_sb[:, list_cols(h)]), y[b][:, cols(h)], MULT)
         for h in range(2):
-            for b in range(2):
-                if (b, h) == (0, 1):
-                    nc.vector.tensor_tensor(yg[b][:, cols(h)], acc[b][h][:], g0[:], MULT)
-                else:
-                    nc.scalar.copy(y[b][:, cols(h)], acc[b][h][:])
-                    nc.vector.tensor_tensor(yg[b][:, cols(h)], gam[b][:].indirect(cls_sb[:, list_cols(h)]), y[b][:, cols(h)], MULT)
-
-        def shift_and_store(b, lo, hi):
-            nc.vector.tensor_tensor(u[b][:, lo:hi], bet[b][:].indirect(cls_sb[:, lo // 16 : hi // 16]), yg[b][:, lo:hi], ADD)
-            nc.scalar.activation(res[b][:, lo:hi], u[b][:, lo:hi], SILU)
-            nc.sync.dma_start(out[b * P : (b + 1) * P, lo:hi], res[b][:, lo:hi])
-
+            for t in range(2):
+                lo = h * HALF + t * P
+                for first, term in ((True, yg[0]), (False, b0)):
+                    nc.tensor.matmul(sums[h][:, t * P : (t + 1) * P], term[:, lo : lo + P], ident[:], start=first, stop=not first, is_transpose=True)
+            nc.scalar.activation(turned[:, cols(h)], sums[h][:], SILU)
         for h in range(2):
-            shift_and_store(0, h * HALF, (h + 1) * HALF)
+            for t in range(2):
+                lo = h * HALF + t * P
+                nc.tensor.transpose(back[h][:, t * P : (t + 1) * P], turned[:, lo : lo + P], ident[:])
+            nc.scalar.copy(res[0][:, cols(h)], back[h][:])
+            nc.sync.dma_start(out[0:P, cols(h)], res[0][:, cols(h)])
         for lo, hi in ((0, 256), (256, 384), (384, 512)):
-            shift_and_store(1, lo, hi)
+            nc.vector.tensor_tensor(u1[:, lo:hi], bet[1][:].indirect(cls_sb[:, lo // 16 : hi // 16]), yg[1][:, lo:hi], ADD)
+            nc.scalar.activation(res[1][:, lo:hi], u1[:, lo:hi], SILU)
+            nc.sync.dma_start(out[P : 2 * P, lo:hi], res[1][:, lo:hi])

@@ -22,8 +22,8 @@ PACK = 4
 PASSES = K // (P * PACK)
 HALF = S // 2
 LAST = 3
-ORDER = ((0, 1, 2, 3), (2, 0, 1, 3))
-CHUNKS = ((0, 640), (640, 1280), (1280, 1792), (1792, 2048))
+ORDER = (2, 0, 1)
+CHUNKS = ((0, 1024), (1024, 1696), (1696, 2048))
 COPY = mybir.ActivationFunctionType.Copy
 LIST_COLS = S // 16
 
@@ -36,9 +36,10 @@ def tile_picked_cbn_silu_e_kernel(tc, xT, w1_words, w1_scales, gamma, beta, offs
 
         offs_sb = keep.tile([P, LIST_COLS], U16, name="offs_sb")
         cls_sb = keep.tile([P, LIST_COLS], U16, name="cls_sb")
-        plane_tiles = [[keep.tile([P, T], F32, name=f"x{z}{j}") for j in range(PACK)] for z in range(PASSES)]
-        planes = [[plane_tiles[z][j][:] for j in range(PACK)] for z in range(PASSES)]
-        w_codes = [keep.tile([P, N], U32, name=f"w_codes{z}", align_bytes=64) for z in range(PASSES)]
+        pairs = [keep.tile([P, 2, T], F32, name=f"pair{u}") for u in range(2)]
+        singles = [keep.tile([P, T], F32, name=f"x1{j}") for j in range(PACK)]
+        planes = [[pairs[j // 2][:, j % 2, :] for j in range(PACK)], [singles[j][:] for j in range(PACK)]]
+        w_codes = keep.tile([P, PASSES, N], U32, name="w_codes", align_bytes=64)
         w_scale = keep.tile([P, N], U8, name="w_scale", align_bytes=64)
         gam = [keep.tile([P, U], F32, name=f"gam{b}") for b in range(2)]
         bet = [keep.tile([P, U], F32, name=f"bet{b}") for b in range(2)]
@@ -53,17 +54,15 @@ def tile_picked_cbn_silu_e_kernel(tc, xT, w1_words, w1_scales, gamma, beta, offs
         for q in range(4):
             nc.gpsimd.dma_start(w_scale[:].bitcast(I32)[32 * q : 32 * q + 4 * PASSES, :], scales_i32[:, 4 * q : 4 * q + 4, :])
 
-        for z in range(PASSES):
-            for j in ORDER[z]:
-                if (z, j) == (PASSES - 1, LAST):
-                    for lo, hi in CHUNKS:
-                        nc.sync.dma_start(plane_tiles[z][j][:, lo:hi], x_rows[z, :, j, lo:hi])
-                else:
-                    nc.sync.dma_start(planes[z][j], x_rows[z, :, j, :])
-                if (z, j) == (0, 0):
-                    nc.sync.dma_start(offs_sb[:], offs)
-        for z in range(PASSES):
-            nc.sync.dma_start(w_codes[z][:].bitcast(I32), w1_words[z].rearrange("p n r -> p (n r)").bitcast(I32))
+        for u in range(2):
+            nc.sync.dma_start(pairs[u][:], x_rows[0, :, 2 * u : 2 * u + 2, :])
+            if u == 0:
+                nc.sync.dma_start(offs_sb[:], offs)
+        for j in ORDER:
+            nc.sync.dma_start(planes[1][j], x_rows[1, :, j, :])
+        for lo, hi in CHUNKS:
+            nc.sync.dma_start(singles[LAST][:, lo:hi], x_rows[1, :, LAST, lo:hi])
+        nc.sync.dma_start(w_codes[:].bitcast(I32), w1_words.rearrange("z p n r -> p z (n r)").bitcast(I32))
         nc.sync.dma_start(cls_sb[:], cls)
         nc.sync.dma_start(bet[0][:], beta[0:P, :])
         nc.sync.dma_start(gam[0][:], gamma[0:P, :])
@@ -73,7 +72,8 @@ def tile_picked_cbn_silu_e_kernel(tc, xT, w1_words, w1_scales, gamma, beta, offs
         picked = [keep.tile([P, S, PACK], BF16, name=f"picked{z}", align_bytes=64) for z in range(PASSES)]
         codes = [keep.tile([P, S], U32, name=f"codes{z}", align_bytes=64) for z in range(PASSES)]
         scale = [keep.tile([P, S], U8, name=f"scale{z}", align_bytes=64) for z in range(PASSES)]
-        acc = [[psum.tile([P, HALF], F32, name=f"acc{b}{h}") for h in range(2)] for b in range(2)]
+        banks = [psum.tile([P, S], F32, name=f"bank{i}") for i in range(4)]
+        acc = [[banks[2 * b + h][:, 0:HALF] for h in range(2)] for b in range(2)]
 
         def cols(h):
             return slice(h * HALF, (h + 1) * HALF)
@@ -91,8 +91,8 @@ def tile_picked_cbn_silu_e_kernel(tc, xT, w1_words, w1_scales, gamma, beta, offs
         def multiply(z, b, h):
             if True:
                 nc.tensor.matmul_mx(
-                    out=acc[b][h][:],
-                    lhsT=w_codes[z][:, b * P : (b + 1) * P].bitcast(FP8X4),
+                    out=acc[b][h],
+                    lhsT=w_codes[:, z, b * P : (b + 1) * P].bitcast(FP8X4),
                     lhsT_scale=w_scale[4 * z :, b * P : (b + 1) * P],
                     rhs=codes[z][:, cols(h)].bitcast(FP8X4),
                     rhs_scale=scale[z][:, cols(h)],
@@ -100,8 +100,13 @@ def tile_picked_cbn_silu_e_kernel(tc, xT, w1_words, w1_scales, gamma, beta, offs
                     stop=(z == PASSES - 1),
                 )
 
-        for j in range(PACK):
+        for j in range(2):
             nc.vector.tensor_copy(picked[0][:, :, j], planes[0][j].indirect(offs_sb[:]))
+        gathered = [keep.tile([P, 2, HALF], F32, name=f"gathered{h}") for h in range(2)]
+        for h in range(2):
+            for j in range(2):
+                nc.vector.tensor_copy(gathered[h][:, j, :], planes[0][2 + j].indirect(offs_sb[:, list_cols(h)]))
+            nc.scalar.copy(picked[0][:, cols(h), 2:4], gathered[h][:].rearrange("p j s -> p s j"))
         quantize(0, 0, S)
         for b in range(2):
             for h in range(2):
@@ -114,10 +119,10 @@ def tile_picked_cbn_silu_e_kernel(tc, xT, w1_words, w1_scales, gamma, beta, offs
         for j in range(2):
             nc.vector.tensor_copy(picked[1][:, :, j], planes[1][j].indirect(offs_sb[:]))
         for c, (lo, hi) in enumerate(CHUNKS):
-            if c == 2:
-                nc.vector.tensor_copy(rounded[:, lo:hi], plane_tiles[1][LAST][:, lo:hi])
+            if c == 1:
+                nc.vector.tensor_copy(rounded[:, lo:hi], singles[LAST][:, lo:hi])
             else:
-                nc.scalar.copy(rounded[:, lo:hi], plane_tiles[1][LAST][:, lo:hi])
+                nc.scalar.copy(rounded[:, lo:hi], singles[LAST][:, lo:hi])
         nc.vector.tensor_copy(picked[1][:, cols(0), LAST], planes[1][LAST].indirect(offs_sb[:, list_cols(0)]))
         nc.scalar.activation(picked[1][:, cols(1), LAST], rounded[:].indirect(offs_sb[:, list_cols(1)]), COPY)
         for h in range(2):
@@ -132,27 +137,25 @@ def tile_picked_cbn_silu_e_kernel(tc, xT, w1_words, w1_scales, gamma, beta, offs
         res = [keep.tile([P, S], F32, name=f"res{b}") for b in range(2)]
         b0 = keep.tile([P, S], F32, name="b0")
         turned = keep.tile([P, S], F32, name="turned")
-        sums = [psum.tile([P, HALF], F32, name=f"sums{h}") for h in range(2)]
-        back = [psum.tile([P, HALF], F32, name=f"back{h}") for h in range(2)]
+        sums = [psum.tile([P, P], F32, name=f"sums{t}") for t in range(4)]
+        back = [banks[h][:, HALF:S] for h in range(2)]
 
         nc.vector.tensor_copy(b0[:], bet[0][:].indirect(cls_sb[:]))
         for b in range(2):
             for h in range(2):
-                nc.scalar.copy(y[b][:, cols(h)], acc[b][h][:])
+                nc.scalar.copy(y[b][:, cols(h)], acc[b][h])
+        for t in range(4):
+            nc.tensor.matmul(sums[t][:], b0[:, t * P : (t + 1) * P], ident[:], start=True, stop=False, is_transpose=True)
         for b in range(2):
-            for h in range(2):
-                nc.vector.tensor_tensor(yg[b][:, cols(h)], gam[b][:].indirect(cls_sb[:, list_cols(h)]), y[b][:, cols(h)], MULT)
+            for lo, hi in (((0, 256), (256, 512)), ((0, 320), (320, 512)))[b]:
+                nc.vector.tensor_tensor(yg[b][:, lo:hi], gam[b][:].indirect(cls_sb[:, lo // 16 : hi // 16]), y[b][:, lo:hi], MULT)
         for h in range(2):
-            for t in range(2):
-                lo = h * HALF + t * P
-                for first, term in ((True, yg[0]), (False, b0)):
-                    nc.tensor.matmul(sums[h][:, t * P : (t + 1) * P], term[:, lo : lo + P], ident[:], start=first, stop=not first, is_transpose=True)
-            nc.scalar.activation(turned[:, cols(h)], sums[h][:], SILU)
-        for h in range(2):
-            for t in range(2):
-                lo = h * HALF + t * P
-                nc.tensor.transpose(back[h][:, t * P : (t + 1) * P], turned[:, lo : lo + P], ident[:])
-            nc.scalar.copy(res[0][:, cols(h)], back[h][:])
+            for t in range(2 * h, 2 * h + 2):
+                nc.tensor.matmul(sums[t][:], yg[0][:, t * P : (t + 1) * P], ident[:], start=False, stop=True, is_transpose=True)
+                nc.scalar.activation(turned[:, t * P : (t + 1) * P], sums[t][:], SILU)
+            for t in range(2 * h, 2 * h + 2):
+                nc.tensor.transpose(back[h][:, (t % 2) * P : (t % 2 + 1) * P], turned[:, t * P : (t + 1) * P], ident[:])
+            nc.scalar.copy(res[0][:, cols(h)], back[h])
             nc.sync.dma_start(out[0:P, cols(h)], res[0][:, cols(h)])
         for lo, hi in ((0, 256), (256, 384), (384, 512)):
             nc.vector.tensor_tensor(u1[:, lo:hi], bet[1][:].indirect(cls_sb[:, lo // 16 : hi // 16]), yg[1][:, lo:hi], ADD)

@@ -23,7 +23,8 @@ PASSES = K // (P * PACK)
 HALF = S // 2
 LAST = 3
 ORDER = (2, 0, 1)
-CHUNKS = ((0, 1024), (1024, 1696), (1696, 2048))
+CHUNKS = ((0, 1536), (1536, 2048))
+CASTS = ((False, 0, 512), (True, 512, 1536), (False, 1536, 1696), (True, 1696, 2048))
 COPY = mybir.ActivationFunctionType.Copy
 LIST_COLS = S // 16
 
@@ -118,8 +119,8 @@ def tile_picked_cbn_silu_e_kernel(tc, xT, w1_words, w1_scales, gamma, beta, offs
         nc.scalar.copy(picked[1][:, cols(1), 2], flat[:])
         for j in range(2):
             nc.vector.tensor_copy(picked[1][:, :, j], planes[1][j].indirect(offs_sb[:]))
-        for c, (lo, hi) in enumerate(CHUNKS):
-            if c == 1:
+        for on_vector, lo, hi in CASTS:
+            if on_vector:
                 nc.vector.tensor_copy(rounded[:, lo:hi], singles[LAST][:, lo:hi])
             else:
                 nc.scalar.copy(rounded[:, lo:hi], singles[LAST][:, lo:hi])

@@ -22,7 +22,7 @@ PACK = 4
 PASSES = K // (P * PACK)
 HALF = S // 2
 LAST = 3
-ORDER = (2, 0, 1)
+ORDER = (0, 1, 2)
 CHUNKS = ((0, 1536), (1536, 2048))
 CASTS = ((False, 0, 512), (True, 512, 1536), (False, 1536, 1696), (True, 1696, 2048))
 COPY = mybir.ActivationFunctionType.Copy
@@ -45,15 +45,15 @@ def tile_picked_cbn_silu_e_kernel(tc, xT, w1_words, w1_scales, gamma, beta, offs
         gam = [keep.tile([P, U], F32, name=f"gam{b}") for b in range(2)]
         bet = [keep.tile([P, U], F32, name=f"bet{b}") for b in range(2)]
 
+        nc.gpsimd.memset(w_scale[:].bitcast(I32), 0)
         ident = keep.tile([P, P], F32, name="ident")
         make_identity(nc, ident[:])
 
         x_rows = xT.rearrange("(z p j) t -> z p j t", z=PASSES, j=PACK)
 
-        nc.gpsimd.memset(w_scale[:].bitcast(I32), 0)
         scales_i32 = w1_scales.bitcast(I32)
         for q in range(4):
-            nc.gpsimd.dma_start(w_scale[:].bitcast(I32)[32 * q : 32 * q + 4 * PASSES, :], scales_i32[:, 4 * q : 4 * q + 4, :])
+            nc.scalar.dma_start(w_scale[:].bitcast(I32)[32 * q : 32 * q + 4 * PASSES, :], scales_i32[:, 4 * q : 4 * q + 4, :])
 
         for u in range(2):
             nc.sync.dma_start(pairs[u][:], x_rows[0, :, 2 * u : 2 * u + 2, :])
@@ -112,13 +112,12 @@ def tile_picked_cbn_silu_e_kernel(tc, xT, w1_words, w1_scales, gamma, beta, offs
         for b in range(2):
             for h in range(2):
                 multiply(0, b, h)
-        flat = keep.tile([P, HALF], BF16, name="flat")
         rounded = keep.tile([P, T], BF16, name="rounded")
-        nc.vector.tensor_copy(picked[1][:, cols(0), 2], planes[1][2].indirect(offs_sb[:, list_cols(0)]))
-        nc.vector.tensor_copy(flat[:], planes[1][2].indirect(offs_sb[:, list_cols(1)]))
-        nc.scalar.copy(picked[1][:, cols(1), 2], flat[:])
-        for j in range(2):
-            nc.vector.tensor_copy(picked[1][:, :, j], planes[1][j].indirect(offs_sb[:]))
+        flat = keep.tile([P, LAST, HALF], F32, name="flat")
+        for j in range(LAST):
+            nc.vector.tensor_copy(flat[:, j, :], planes[1][j].indirect(offs_sb[:, list_cols(1)]))
+            nc.vector.tensor_copy(picked[1][:, cols(0), j], planes[1][j].indirect(offs_sb[:, list_cols(0)]))
+        nc.scalar.copy(picked[1][:, cols(1), 0:LAST], flat[:].rearrange("p j s -> p s j"))
         for on_vector, lo, hi in CASTS:
             if on_vector:
                 nc.vector.tensor_copy(rounded[:, lo:hi], singles[LAST][:, lo:hi])

@@ -16,17 +16,18 @@ FP8X4 = mybir.dt.float8_e4m3fn_x4
 MULT = mybir.AluOpType.mult
 ADD = mybir.AluOpType.add
 SILU = mybir.ActivationFunctionType.Silu
+COPY = mybir.ActivationFunctionType.Copy
 
 P = 128
 PACK = 4
 PASSES = K // (P * PACK)
+BLOCKS = N // P
 HALF = S // 2
-LAST = 3
-ORDER = (0, 1, 2)
-CHUNKS = ((0, 1536), (1536, 2048))
-CASTS = ((False, 0, 512), (True, 512, 1536), (False, 1536, 1696), (True, 1696, 2048))
-COPY = mybir.ActivationFunctionType.Copy
-LIST_COLS = S // 16
+LAST = PACK - 1
+CUT = 1536
+SCALAR_CAST = 576
+HALVES = ((0, HALF), (HALF, S))
+ENDS = ((0, 192), (192, 384), (384, 512))
 
 
 def tile_picked_cbn_silu_e_kernel(tc, xT, w1_words, w1_scales, gamma, beta, offs, cls, out):
@@ -35,129 +36,115 @@ def tile_picked_cbn_silu_e_kernel(tc, xT, w1_words, w1_scales, gamma, beta, offs
         keep = ctx.enter_context(tc.tile_pool(name="keep", bufs=1))
         psum = ctx.enter_context(tc.psum_pool(name="psum", bufs=1))
 
-        offs_sb = keep.tile([P, LIST_COLS], U16, name="offs_sb")
-        cls_sb = keep.tile([P, LIST_COLS], U16, name="cls_sb")
+        offs_sb = keep.tile([P, S // 16], U16, name="offs_sb")
+        cls_sb = keep.tile([P, S // 16], U16, name="cls_sb")
         pairs = [keep.tile([P, 2, T], F32, name=f"pair{u}") for u in range(2)]
-        singles = [keep.tile([P, T], F32, name=f"x1{j}") for j in range(PACK)]
-        planes = [[pairs[j // 2][:, j % 2, :] for j in range(PACK)], [singles[j][:] for j in range(PACK)]]
+        singles = [keep.tile([P, T], F32, name=f"single{j}") for j in range(PACK)]
         w_codes = keep.tile([P, PASSES, N], U32, name="w_codes", align_bytes=64)
         w_scale = keep.tile([P, N], U8, name="w_scale", align_bytes=64)
-        gam = [keep.tile([P, U], F32, name=f"gam{b}") for b in range(2)]
-        bet = [keep.tile([P, U], F32, name=f"bet{b}") for b in range(2)]
+        gam = [keep.tile([P, U], F32, name=f"gam{b}") for b in range(BLOCKS)]
+        bet = [keep.tile([P, U], F32, name=f"bet{b}") for b in range(BLOCKS)]
 
-        nc.gpsimd.memset(w_scale[:].bitcast(I32), 0)
+        nc.vector.memset(w_scale[:].bitcast(I32), 0)
         ident = keep.tile([P, P], F32, name="ident")
         make_identity(nc, ident[:])
-
-        x_rows = xT.rearrange("(z p j) t -> z p j t", z=PASSES, j=PACK)
-
+        warm = keep.tile([P, 1], F32, name="warm")
+        nc.scalar.activation(warm[:], ident[:, 0:1], SILU)
         scales_i32 = w1_scales.bitcast(I32)
         for q in range(4):
             nc.scalar.dma_start(w_scale[:].bitcast(I32)[32 * q : 32 * q + 4 * PASSES, :], scales_i32[:, 4 * q : 4 * q + 4, :])
 
+        x_rows = xT.rearrange("(z p j) t -> z p j t", z=PASSES, j=PACK)
         for u in range(2):
             nc.sync.dma_start(pairs[u][:], x_rows[0, :, 2 * u : 2 * u + 2, :])
             if u == 0:
                 nc.sync.dma_start(offs_sb[:], offs)
-        for j in ORDER:
-            nc.sync.dma_start(planes[1][j], x_rows[1, :, j, :])
-        for lo, hi in CHUNKS:
-            nc.sync.dma_start(singles[LAST][:, lo:hi], x_rows[1, :, LAST, lo:hi])
-        nc.sync.dma_start(w_codes[:].bitcast(I32), w1_words.rearrange("z p n r -> p z (n r)").bitcast(I32))
+        for j in range(LAST):
+            nc.sync.dma_start(singles[j][:], x_rows[1, :, j, :])
         nc.sync.dma_start(cls_sb[:], cls)
+        for lo, hi in ((0, CUT), (CUT, T)):
+            nc.sync.dma_start(singles[LAST][:, lo:hi], x_rows[1, :, LAST, lo:hi])
         nc.sync.dma_start(bet[0][:], beta[0:P, :])
-        nc.sync.dma_start(gam[0][:], gamma[0:P, :])
-        nc.sync.dma_start(gam[1][:], gamma[P : 2 * P, :])
-        nc.sync.dma_start(bet[1][:], beta[P : 2 * P, :])
+        nc.sync.dma_start(w_codes[:].bitcast(I32), w1_words.rearrange("z p n r -> p z (n r)").bitcast(I32))
+        for b in range(BLOCKS):
+            nc.sync.dma_start(gam[b][:], gamma[b * P : (b + 1) * P, :])
+        nc.sync.dma_start(bet[1][:], beta[P:N, :])
 
-        picked = [keep.tile([P, S, PACK], BF16, name=f"picked{z}", align_bytes=64) for z in range(PASSES)]
+        picked0 = keep.tile([P, S, PACK], BF16, name="picked0", align_bytes=64)
+        picked1 = [keep.tile([P, HALF, PACK], BF16, name=f"picked1{h}", tag=f"half{h}", align_bytes=64) for h in range(2)]
         codes = [keep.tile([P, S], U32, name=f"codes{z}", align_bytes=64) for z in range(PASSES)]
         scale = [keep.tile([P, S], U8, name=f"scale{z}", align_bytes=64) for z in range(PASSES)]
-        banks = [psum.tile([P, S], F32, name=f"bank{i}") for i in range(4)]
-        acc = [[banks[2 * b + h][:, 0:HALF] for h in range(2)] for b in range(2)]
 
-        def cols(h):
-            return slice(h * HALF, (h + 1) * HALF)
+        def by_offs(window, lo, hi):
+            return window.indirect(offs_sb[:, lo // 16 : hi // 16])
 
-        def list_cols(h):
-            return slice(h * LIST_COLS // 2, (h + 1) * LIST_COLS // 2)
+        def by_cls(window, lo, hi):
+            return window.indirect(cls_sb[:, lo // 16 : hi // 16])
 
-        def quantize(z, lo, hi):
+        def quantize(z, lo, hi, values):
             nc.vector.quantize_mx(
                 out=codes[z][:, lo:hi].bitcast(FP8X4),
                 scales=scale[z][:, lo:hi],
-                in_=picked[z][:, lo:hi, :].rearrange("p s j -> p (s j)"),
+                in_=values.rearrange("p s j -> p (s j)"),
             )
 
-        def multiply(z, b, h):
-            if True:
-                nc.tensor.matmul_mx(
-                    out=acc[b][h],
-                    lhsT=w_codes[:, z, b * P : (b + 1) * P].bitcast(FP8X4),
-                    lhsT_scale=w_scale[4 * z :, b * P : (b + 1) * P],
-                    rhs=codes[z][:, cols(h)].bitcast(FP8X4),
-                    rhs_scale=scale[z][:, cols(h)],
-                    start=(z == 0),
-                    stop=(z == PASSES - 1),
-                )
+        for j in range(PACK):
+            nc.vector.tensor_copy(picked0[:, :, j], by_offs(pairs[j // 2][:, j % 2, :], 0, S))
+        quantize(0, 0, S, picked0[:])
 
-        for j in range(2):
-            nc.vector.tensor_copy(picked[0][:, :, j], planes[0][j].indirect(offs_sb[:]))
-        gathered = [keep.tile([P, 2, HALF], F32, name=f"gathered{h}") for h in range(2)]
-        for h in range(2):
-            for j in range(2):
-                nc.vector.tensor_copy(gathered[h][:, j, :], planes[0][2 + j].indirect(offs_sb[:, list_cols(h)]))
-            nc.scalar.copy(picked[0][:, cols(h), 2:4], gathered[h][:].rearrange("p j s -> p s j"))
-        quantize(0, 0, S)
-        for b in range(2):
-            for h in range(2):
-                multiply(0, b, h)
-        rounded = keep.tile([P, T], BF16, name="rounded")
         flat = keep.tile([P, LAST, HALF], F32, name="flat")
+        rounded = keep.tile([P, T], BF16, name="rounded", tag="sums0")
         for j in range(LAST):
-            nc.vector.tensor_copy(flat[:, j, :], planes[1][j].indirect(offs_sb[:, list_cols(1)]))
-            nc.vector.tensor_copy(picked[1][:, cols(0), j], planes[1][j].indirect(offs_sb[:, list_cols(0)]))
-        nc.scalar.copy(picked[1][:, cols(1), 0:LAST], flat[:].rearrange("p j s -> p s j"))
-        for on_vector, lo, hi in CASTS:
-            if on_vector:
-                nc.vector.tensor_copy(rounded[:, lo:hi], singles[LAST][:, lo:hi])
-            else:
-                nc.scalar.copy(rounded[:, lo:hi], singles[LAST][:, lo:hi])
-        nc.vector.tensor_copy(picked[1][:, cols(0), LAST], planes[1][LAST].indirect(offs_sb[:, list_cols(0)]))
-        nc.scalar.activation(picked[1][:, cols(1), LAST], rounded[:].indirect(offs_sb[:, list_cols(1)]), COPY)
-        for h in range(2):
-            quantize(1, h * HALF, (h + 1) * HALF)
-        for b in range(2):
-            for h in range(2):
-                multiply(1, b, h)
+            nc.vector.tensor_copy(flat[:, j, :], by_offs(singles[j][:], HALF, S))
+            nc.vector.tensor_copy(picked1[0][:, :, j], by_offs(singles[j][:], 0, HALF))
+        nc.scalar.copy(picked1[1][:, :, 0:LAST], flat[:].rearrange("p j s -> p s j"))
+        nc.scalar.copy(rounded[:, 0:SCALAR_CAST], singles[LAST][:, 0:SCALAR_CAST])
+        nc.vector.tensor_copy(rounded[:, SCALAR_CAST:CUT], singles[LAST][:, SCALAR_CAST:CUT])
+        nc.scalar.copy(rounded[:, CUT:T], singles[LAST][:, CUT:T])
+        nc.vector.tensor_copy(picked1[0][:, :, LAST], by_offs(singles[LAST][:], 0, HALF))
+        nc.scalar.activation(picked1[1][:, :, LAST], by_offs(rounded[:], HALF, S), COPY)
+        shift0 = keep.tile([P, S], F32, name="shift0")
+        for h, (lo, hi) in enumerate(HALVES):
+            quantize(1, lo, hi, picked1[h][:])
+            nc.vector.tensor_copy(shift0[:, lo:hi], by_cls(bet[0][:], lo, hi))
 
-        y = [keep.tile([P, S], F32, name=f"y{b}") for b in range(2)]
-        yg = [keep.tile([P, S], F32, name=f"yg{b}") for b in range(2)]
-        u1 = keep.tile([P, S], F32, name="u1")
-        res = [keep.tile([P, S], F32, name=f"res{b}") for b in range(2)]
-        b0 = keep.tile([P, S], F32, name="b0")
+        y = [keep.tile([P, S], F32, name=f"y{b}", tag=f"sums{b}") for b in range(BLOCKS)]
+        for b in range(BLOCKS):
+            for h, (lo, hi) in enumerate(HALVES):
+                acc = psum.tile([P, HALF], F32, name=f"acc{b}{h}", tag=f"bank{b}{h}")
+                for z in range(PASSES):
+                    nc.tensor.matmul_mx(
+                        out=acc[:],
+                        lhsT=w_codes[:, z, b * P : (b + 1) * P].bitcast(FP8X4),
+                        lhsT_scale=w_scale[4 * z :, b * P : (b + 1) * P],
+                        rhs=codes[z][:, lo:hi].bitcast(FP8X4),
+                        rhs_scale=scale[z][:, lo:hi],
+                        start=(z == 0),
+                        stop=(z == PASSES - 1),
+                    )
+                nc.scalar.copy(y[b][:, lo:hi], acc[:])
+
+        scaled = [keep.tile([P, S], F32, name=f"scaled{b}") for b in range(BLOCKS)]
+        res = [keep.tile([P, S], F32, name=f"res{b}") for b in range(BLOCKS)]
         turned = keep.tile([P, S], F32, name="turned")
-        sums = [psum.tile([P, P], F32, name=f"sums{t}") for t in range(4)]
-        back = [banks[h][:, HALF:S] for h in range(2)]
+        for h, (lo, hi) in enumerate(HALVES):
+            sums = psum.tile([P, HALF], F32, name=f"sums{h}", tag=f"bank0{h}")
+            back = psum.tile([P, HALF], F32, name=f"back{h}")
+            for c in range(lo, hi, P):
+                nc.tensor.matmul(sums[:, c - lo : c - lo + P], shift0[:, c : c + P], ident[:], start=(c == lo), stop=False, is_transpose=True)
+            nc.vector.tensor_tensor(scaled[0][:, lo:hi], by_cls(gam[0][:], lo, hi), y[0][:, lo:hi], MULT)
+            for c in range(lo, hi, P):
+                nc.tensor.matmul(sums[:, c - lo : c - lo + P], scaled[0][:, c : c + P], ident[:], start=False, stop=(c == hi - P), is_transpose=True)
+            nc.scalar.activation(turned[:, lo:hi], sums[:], SILU)
+            for c in range(lo, hi, P):
+                nc.tensor.transpose(back[:, c - lo : c - lo + P], turned[:, c : c + P], ident[:])
+            nc.scalar.copy(res[0][:, lo:hi], back[:])
+            nc.sync.dma_start(out[0:P, lo:hi], res[0][:, lo:hi])
 
-        nc.vector.tensor_copy(b0[:], bet[0][:].indirect(cls_sb[:]))
-        for b in range(2):
-            for h in range(2):
-                nc.scalar.copy(y[b][:, cols(h)], acc[b][h])
-        for t in range(4):
-            nc.tensor.matmul(sums[t][:], b0[:, t * P : (t + 1) * P], ident[:], start=True, stop=False, is_transpose=True)
-        for b in range(2):
-            for lo, hi in (((0, 256), (256, 512)), ((0, 320), (320, 512)))[b]:
-                nc.vector.tensor_tensor(yg[b][:, lo:hi], gam[b][:].indirect(cls_sb[:, lo // 16 : hi // 16]), y[b][:, lo:hi], MULT)
-        for h in range(2):
-            for t in range(2 * h, 2 * h + 2):
-                nc.tensor.matmul(sums[t][:], yg[0][:, t * P : (t + 1) * P], ident[:], start=False, stop=True, is_transpose=True)
-                nc.scalar.activation(turned[:, t * P : (t + 1) * P], sums[t][:], SILU)
-            for t in range(2 * h, 2 * h + 2):
-                nc.tensor.transpose(back[h][:, (t % 2) * P : (t % 2 + 1) * P], turned[:, t * P : (t + 1) * P], ident[:])
-            nc.scalar.copy(res[0][:, cols(h)], back[h])
-            nc.sync.dma_start(out[0:P, cols(h)], res[0][:, cols(h)])
-        for lo, hi in ((0, 256), (256, 384), (384, 512)):
-            nc.vector.tensor_tensor(u1[:, lo:hi], bet[1][:].indirect(cls_sb[:, lo // 16 : hi // 16]), yg[1][:, lo:hi], ADD)
-            nc.scalar.activation(res[1][:, lo:hi], u1[:, lo:hi], SILU)
-            nc.sync.dma_start(out[P : 2 * P, lo:hi], res[1][:, lo:hi])
+        shifted = keep.tile([P, S], F32, name="shifted")
+        for lo, hi in HALVES:
+            nc.vector.tensor_tensor(scaled[1][:, lo:hi], by_cls(gam[1][:], lo, hi), y[1][:, lo:hi], MULT)
+        for lo, hi in ENDS:
+            nc.vector.tensor_tensor(shifted[:, lo:hi], by_cls(bet[1][:], lo, hi), scaled[1][:, lo:hi], ADD)
+            nc.scalar.activation(res[1][:, lo:hi], shifted[:, lo:hi], SILU)
+            nc.sync.dma_start(out[P:N, lo:hi], res[1][:, lo:hi])

@@ -25,7 +25,7 @@ BLOCKS = N // P
 HALF = S // 2
 LAST = PACK - 1
 CUT = 1536
-SCALAR_CAST = 576
+SCALAR_CASTS = (512, 160)
 HALVES = ((0, HALF), (HALF, S))
 ENDS = ((0, 192), (192, 384), (384, 512))
 
@@ -39,7 +39,7 @@ def tile_picked_cbn_silu_e_kernel(tc, xT, w1_words, w1_scales, gamma, beta, offs
         offs_sb = keep.tile([P, S // 16], U16, name="offs_sb")
         cls_sb = keep.tile([P, S // 16], U16, name="cls_sb")
         pairs = [keep.tile([P, 2, T], F32, name=f"pair{u}") for u in range(2)]
-        singles = [keep.tile([P, T], F32, name=f"single{j}") for j in range(PACK)]
+        singles = [keep.tile([P, T], F32, name=f"single{j}", tag=f"single{j}", align_bytes=64) for j in range(PACK)]
         w_codes = keep.tile([P, PASSES, N], U32, name="w_codes", align_bytes=64)
         w_scale = keep.tile([P, N], U8, name="w_scale", align_bytes=64)
         gam = [keep.tile([P, U], F32, name=f"gam{b}") for b in range(BLOCKS)]
@@ -61,18 +61,17 @@ def tile_picked_cbn_silu_e_kernel(tc, xT, w1_words, w1_scales, gamma, beta, offs
                 nc.sync.dma_start(offs_sb[:], offs)
         for j in range(LAST):
             nc.sync.dma_start(singles[j][:], x_rows[1, :, j, :])
-        nc.sync.dma_start(cls_sb[:], cls)
         for lo, hi in ((0, CUT), (CUT, T)):
             nc.sync.dma_start(singles[LAST][:, lo:hi], x_rows[1, :, LAST, lo:hi])
-        nc.sync.dma_start(bet[0][:], beta[0:P, :])
         nc.sync.dma_start(w_codes[:].bitcast(I32), w1_words.rearrange("z p n r -> p z (n r)").bitcast(I32))
+        nc.sync.dma_start(cls_sb[:], cls)
+        nc.sync.dma_start(bet[0][:], beta[0:P, :])
         for b in range(BLOCKS):
             nc.sync.dma_start(gam[b][:], gamma[b * P : (b + 1) * P, :])
         nc.sync.dma_start(bet[1][:], beta[P:N, :])
 
         picked0 = keep.tile([P, S, PACK], BF16, name="picked0", align_bytes=64)
         picked1 = [keep.tile([P, HALF, PACK], BF16, name=f"picked1{h}", tag=f"half{h}", align_bytes=64) for h in range(2)]
-        codes = [keep.tile([P, S], U32, name=f"codes{z}", align_bytes=64) for z in range(PASSES)]
         scale = [keep.tile([P, S], U8, name=f"scale{z}", align_bytes=64) for z in range(PASSES)]
 
         def by_offs(window, lo, hi):
@@ -88,33 +87,42 @@ def tile_picked_cbn_silu_e_kernel(tc, xT, w1_words, w1_scales, gamma, beta, offs
                 in_=values.rearrange("p s j -> p (s j)"),
             )
 
-        for j in range(PACK):
-            nc.vector.tensor_copy(picked0[:, :, j], by_offs(pairs[j // 2][:, j % 2, :], 0, S))
-        quantize(0, 0, S, picked0[:])
+        for j in range(2):
+            nc.vector.tensor_copy(picked0[:, :, j], by_offs(pairs[0][:, j, :], 0, S))
+        for h, (lo, hi) in enumerate(HALVES):
+            flat0 = keep.tile([P, 2, HALF], F32, name=f"flat0{h}")
+            for j in range(2):
+                nc.vector.tensor_copy(flat0[:, j, :], by_offs(pairs[1][:, j, :], lo, hi))
+            nc.scalar.copy(picked0[:, lo:hi, 2:4], flat0[:].rearrange("p j s -> p s j"))
 
-        flat = keep.tile([P, LAST, HALF], F32, name="flat")
+        flat1 = keep.tile([P, LAST, S], F32, name="flat1")
         rounded = keep.tile([P, T], BF16, name="rounded", tag="sums0")
-        for j in range(LAST):
-            nc.vector.tensor_copy(flat[:, j, :], by_offs(singles[j][:], HALF, S))
-            nc.vector.tensor_copy(picked1[0][:, :, j], by_offs(singles[j][:], 0, HALF))
-        nc.scalar.copy(picked1[1][:, :, 0:LAST], flat[:].rearrange("p j s -> p s j"))
-        nc.scalar.copy(rounded[:, 0:SCALAR_CAST], singles[LAST][:, 0:SCALAR_CAST])
-        nc.vector.tensor_copy(rounded[:, SCALAR_CAST:CUT], singles[LAST][:, SCALAR_CAST:CUT])
-        nc.scalar.copy(rounded[:, CUT:T], singles[LAST][:, CUT:T])
+        nc.vector.tensor_copy(flat1[:, 0, :], by_offs(singles[0][:], 0, S))
+        codes = [keep.tile([P, S], U32, name="codes0", tag="single0", align_bytes=64)]
+        quantize(0, 0, S, picked0[:])
+        nc.vector.tensor_copy(flat1[:, 1, :], by_offs(singles[1][:], 0, S))
+        nc.scalar.copy(picked1[0][:, :, 0:2], flat1[:, 0:2, 0:HALF].rearrange("p j s -> p s j"))
+        nc.vector.tensor_copy(flat1[:, 2, HALF:S], by_offs(singles[2][:], HALF, S))
+        nc.vector.tensor_copy(picked1[0][:, :, 2], by_offs(singles[2][:], 0, HALF))
+        nc.scalar.copy(picked1[1][:, :, 0:LAST], flat1[:, :, HALF:S].rearrange("p j s -> p s j"))
+        for (lo, hi), share in zip(((0, CUT), (CUT, T)), SCALAR_CASTS):
+            nc.scalar.copy(rounded[:, lo : lo + share], singles[LAST][:, lo : lo + share])
+            nc.vector.tensor_copy(rounded[:, lo + share : hi], singles[LAST][:, lo + share : hi])
         nc.vector.tensor_copy(picked1[0][:, :, LAST], by_offs(singles[LAST][:], 0, HALF))
         nc.scalar.activation(picked1[1][:, :, LAST], by_offs(rounded[:], HALF, S), COPY)
+        codes.append(keep.tile([P, S], U32, name="codes1", align_bytes=64))
         shift0 = keep.tile([P, S], F32, name="shift0")
         for h, (lo, hi) in enumerate(HALVES):
             quantize(1, lo, hi, picked1[h][:])
-            nc.vector.tensor_copy(shift0[:, lo:hi], by_cls(bet[0][:], lo, hi))
+        nc.vector.tensor_copy(shift0[:], by_cls(bet[0][:], 0, S))
 
         y = [keep.tile([P, S], F32, name=f"y{b}", tag=f"sums{b}") for b in range(BLOCKS)]
-        for b in range(BLOCKS):
-            for h, (lo, hi) in enumerate(HALVES):
-                acc = psum.tile([P, HALF], F32, name=f"acc{b}{h}", tag=f"bank{b}{h}")
-                for z in range(PASSES):
+        acc = [[psum.tile([P, HALF], F32, name=f"acc{b}{h}", tag=f"bank{b}{h}") for h in range(2)] for b in range(BLOCKS)]
+        for z in range(PASSES):
+            for b in range(BLOCKS):
+                for h, (lo, hi) in enumerate(HALVES):
                     nc.tensor.matmul_mx(
-                        out=acc[:],
+                        out=acc[b][h][:],
                         lhsT=w_codes[:, z, b * P : (b + 1) * P].bitcast(FP8X4),
                         lhsT_scale=w_scale[4 * z :, b * P : (b + 1) * P],
                         rhs=codes[z][:, lo:hi].bitcast(FP8X4),
@@ -122,7 +130,9 @@ def tile_picked_cbn_silu_e_kernel(tc, xT, w1_words, w1_scales, gamma, beta, offs
                         start=(z == 0),
                         stop=(z == PASSES - 1),
                     )
-                nc.scalar.copy(y[b][:, lo:hi], acc[:])
+        for b in range(BLOCKS):
+            for h, (lo, hi) in enumerate(HALVES):
+                nc.scalar.copy(y[b][:, lo:hi], acc[b][h][:])
 
         scaled = [keep.tile([P, S], F32, name=f"scaled{b}") for b in range(BLOCKS)]
         res = [keep.tile([P, S], F32, name=f"res{b}") for b in range(BLOCKS)]

@@ -50,9 +50,6 @@ def tile_picked_cbn_silu_e_kernel(tc, xT, w1_words, w1_scales, gamma, beta, offs
         make_identity(nc, ident[:])
         warm = keep.tile([P, 1], F32, name="warm")
         nc.scalar.activation(warm[:], ident[:, 0:1], SILU)
-        scales_i32 = w1_scales.bitcast(I32)
-        for q in range(4):
-            nc.scalar.dma_start(w_scale[:].bitcast(I32)[32 * q : 32 * q + 4 * PASSES, :], scales_i32[:, 4 * q : 4 * q + 4, :])
 
         x_rows = xT.rearrange("(z p j) t -> z p j t", z=PASSES, j=PACK)
         for u in range(2):
@@ -63,9 +60,12 @@ def tile_picked_cbn_silu_e_kernel(tc, xT, w1_words, w1_scales, gamma, beta, offs
             nc.sync.dma_start(singles[j][:], x_rows[1, :, j, :])
         for lo, hi in ((0, CUT), (CUT, T)):
             nc.sync.dma_start(singles[LAST][:, lo:hi], x_rows[1, :, LAST, lo:hi])
+        scales_i32 = w1_scales.bitcast(I32)
+        for q in range(4):
+            nc.sync.dma_start(w_scale[:].bitcast(I32)[32 * q : 32 * q + 4 * PASSES, :], scales_i32[:, 4 * q : 4 * q + 4, :])
         nc.sync.dma_start(w_codes[:].bitcast(I32), w1_words.rearrange("z p n r -> p z (n r)").bitcast(I32))
-        nc.sync.dma_start(cls_sb[:], cls)
         nc.sync.dma_start(bet[0][:], beta[0:P, :])
+        nc.sync.dma_start(cls_sb[:], cls)
         for b in range(BLOCKS):
             nc.sync.dma_start(gam[b][:], gamma[b * P : (b + 1) * P, :])
         nc.sync.dma_start(bet[1][:], beta[P:N, :])

@@ -24,8 +24,8 @@ PASSES = K // (P * PACK)
 BLOCKS = N // P
 HALF = S // 2
 LAST = PACK - 1
-CUT = 1536
-SCALAR_CASTS = (512, 160)
+CUT = 1408
+SCALAR_CAST = 528
 HALVES = ((0, HALF), (HALF, S))
 ENDS = ((0, 192), (192, 384), (384, 512))
 
@@ -58,14 +58,14 @@ def tile_picked_cbn_silu_e_kernel(tc, xT, w1_words, w1_scales, gamma, beta, offs
                 nc.sync.dma_start(offs_sb[:], offs)
         for j in range(LAST):
             nc.sync.dma_start(singles[j][:], x_rows[1, :, j, :])
+        nc.sync.dma_start(cls_sb[:], cls)
         for lo, hi in ((0, CUT), (CUT, T)):
             nc.sync.dma_start(singles[LAST][:, lo:hi], x_rows[1, :, LAST, lo:hi])
+        nc.sync.dma_start(bet[0][:], beta[0:P, :])
         scales_i32 = w1_scales.bitcast(I32)
         for q in range(4):
             nc.sync.dma_start(w_scale[:].bitcast(I32)[32 * q : 32 * q + 4 * PASSES, :], scales_i32[:, 4 * q : 4 * q + 4, :])
         nc.sync.dma_start(w_codes[:].bitcast(I32), w1_words.rearrange("z p n r -> p z (n r)").bitcast(I32))
-        nc.sync.dma_start(bet[0][:], beta[0:P, :])
-        nc.sync.dma_start(cls_sb[:], cls)
         for b in range(BLOCKS):
             nc.sync.dma_start(gam[b][:], gamma[b * P : (b + 1) * P, :])
         nc.sync.dma_start(bet[1][:], beta[P:N, :])
@@ -105,22 +105,23 @@ def tile_picked_cbn_silu_e_kernel(tc, xT, w1_words, w1_scales, gamma, beta, offs
         nc.vector.tensor_copy(flat1[:, 2, HALF:S], by_offs(singles[2][:], HALF, S))
         nc.vector.tensor_copy(picked1[0][:, :, 2], by_offs(singles[2][:], 0, HALF))
         nc.scalar.copy(picked1[1][:, :, 0:LAST], flat1[:, :, HALF:S].rearrange("p j s -> p s j"))
-        for (lo, hi), share in zip(((0, CUT), (CUT, T)), SCALAR_CASTS):
-            nc.scalar.copy(rounded[:, lo : lo + share], singles[LAST][:, lo : lo + share])
-            nc.vector.tensor_copy(rounded[:, lo + share : hi], singles[LAST][:, lo + share : hi])
+        nc.scalar.copy(rounded[:, 0:SCALAR_CAST], singles[LAST][:, 0:SCALAR_CAST])
+        nc.vector.tensor_copy(rounded[:, SCALAR_CAST:CUT], singles[LAST][:, SCALAR_CAST:CUT])
+        nc.scalar.copy(rounded[:, CUT:T], singles[LAST][:, CUT:T])
         nc.vector.tensor_copy(picked1[0][:, :, LAST], by_offs(singles[LAST][:], 0, HALF))
         nc.scalar.activation(picked1[1][:, :, LAST], by_offs(rounded[:], HALF, S), COPY)
         codes.append(keep.tile([P, S], U32, name="codes1", align_bytes=64))
-        shift0 = keep.tile([P, S], F32, name="shift0")
+        shift0 = []
         for h, (lo, hi) in enumerate(HALVES):
             quantize(1, lo, hi, picked1[h][:])
-        nc.vector.tensor_copy(shift0[:], by_cls(bet[0][:], 0, S))
+            shift0.append(keep.tile([P, HALF], F32, name=f"shift0{h}", tag=("shift00", "half1")[h], align_bytes=64))
+            nc.vector.tensor_copy(shift0[h][:], by_cls(bet[0][:], lo, hi))
 
         y = [keep.tile([P, S], F32, name=f"y{b}", tag=f"sums{b}") for b in range(BLOCKS)]
         acc = [[psum.tile([P, HALF], F32, name=f"acc{b}{h}", tag=f"bank{b}{h}") for h in range(2)] for b in range(BLOCKS)]
-        for z in range(PASSES):
-            for b in range(BLOCKS):
-                for h, (lo, hi) in enumerate(HALVES):
+        for b in range(BLOCKS):
+            for h, (lo, hi) in enumerate(HALVES):
+                for z in range(PASSES):
                     nc.tensor.matmul_mx(
                         out=acc[b][h][:],
                         lhsT=w_codes[:, z, b * P : (b + 1) * P].bitcast(FP8X4),
@@ -141,7 +142,7 @@ def tile_picked_cbn_silu_e_kernel(tc, xT, w1_words, w1_scales, gamma, beta, offs
             sums = psum.tile([P, HALF], F32, name=f"sums{h}", tag=f"bank0{h}")
             back = psum.tile([P, HALF], F32, name=f"back{h}")
             for c in range(lo, hi, P):
-                nc.tensor.matmul(sums[:, c - lo : c - lo + P], shift0[:, c : c + P], ident[:], start=(c == lo), stop=False, is_transpose=True)
+                nc.tensor.matmul(sums[:, c - lo : c - lo + P], shift0[h][:, c - lo : c - lo + P], ident[:], start=(c == lo), stop=False, is_transpose=True)
             nc.vector.tensor_tensor(scaled[0][:, lo:hi], by_cls(gam[0][:], lo, hi), y[0][:, lo:hi], MULT)
             for c in range(lo, hi, P):
                 nc.tensor.matmul(sums[:, c - lo : c - lo + P], scaled[0][:, c : c + P], ident[:], start=False, stop=(c == hi - P), is_transpose=True)

@@ -27,7 +27,7 @@ LAST = PACK - 1
 CUT = 1408
 SCALAR_CAST = 528
 HALVES = ((0, HALF), (HALF, S))
-ENDS = ((0, 192), (192, 384), (384, 512))
+ENDS = ((0, 256), (256, 384), (384, 512))
 
 
 def tile_picked_cbn_silu_e_kernel(tc, xT, w1_words, w1_scales, gamma, beta, offs, cls, out):
@@ -40,7 +40,7 @@ def tile_picked_cbn_silu_e_kernel(tc, xT, w1_words, w1_scales, gamma, beta, offs
         cls_sb = keep.tile([P, S // 16], U16, name="cls_sb")
         pairs = [keep.tile([P, 2, T], F32, name=f"pair{u}") for u in range(2)]
         singles = [keep.tile([P, T], F32, name=f"single{j}", tag=f"single{j}", align_bytes=64) for j in range(PACK)]
-        w_codes = keep.tile([P, PASSES, N], U32, name="w_codes", align_bytes=64)
+        w_codes = [keep.tile([P, PASSES, P], U32, name=f"w_codes{b}", align_bytes=64) for b in range(BLOCKS)]
         w_scale = keep.tile([P, N], U8, name="w_scale", align_bytes=64)
         gam = [keep.tile([P, U], F32, name=f"gam{b}") for b in range(BLOCKS)]
         bet = [keep.tile([P, U], F32, name=f"bet{b}") for b in range(BLOCKS)]
@@ -65,7 +65,9 @@ def tile_picked_cbn_silu_e_kernel(tc, xT, w1_words, w1_scales, gamma, beta, offs
         scales_i32 = w1_scales.bitcast(I32)
         for q in range(4):
             nc.sync.dma_start(w_scale[:].bitcast(I32)[32 * q : 32 * q + 4 * PASSES, :], scales_i32[:, 4 * q : 4 * q + 4, :])
-        nc.sync.dma_start(w_codes[:].bitcast(I32), w1_words.rearrange("z p n r -> p z (n r)").bitcast(I32))
+        w_rows = w1_words.rearrange("z p n r -> p z (n r)").bitcast(I32)
+        for b in range(BLOCKS):
+            nc.sync.dma_start(w_codes[b][:].bitcast(I32), w_rows[:, :, b * P : (b + 1) * P])
         for b in range(BLOCKS):
             nc.sync.dma_start(gam[b][:], gamma[b * P : (b + 1) * P, :])
         nc.sync.dma_start(bet[1][:], beta[P:N, :])
@@ -124,7 +126,7 @@ def tile_picked_cbn_silu_e_kernel(tc, xT, w1_words, w1_scales, gamma, beta, offs
                 for z in range(PASSES):
                     nc.tensor.matmul_mx(
                         out=acc[b][h][:],
-                        lhsT=w_codes[:, z, b * P : (b + 1) * P].bitcast(FP8X4),
+                        lhsT=w_codes[b][:, z, :].bitcast(FP8X4),
                         lhsT_scale=w_scale[4 * z :, b * P : (b + 1) * P],
                         rhs=codes[z][:, lo:hi].bitcast(FP8X4),
                         rhs_scale=scale[z][:, lo:hi],

@@ -24,8 +24,9 @@ PASSES = K // (P * PACK)
 BLOCKS = N // P
 HALF = S // 2
 LAST = PACK - 1
-CUT = 1408
-SCALAR_CAST = 528
+CHUNKS = ((0, 1152), (1152, 1664), (1664, T))
+SCALAR_HEAD = 512
+VECTOR_END = 1856
 HALVES = ((0, HALF), (HALF, S))
 ENDS = ((0, 256), (256, 384), (384, 512))
 
@@ -40,7 +41,7 @@ def tile_picked_cbn_silu_e_kernel(tc, xT, w1_words, w1_scales, gamma, beta, offs
         cls_sb = keep.tile([P, S // 16], U16, name="cls_sb")
         pairs = [keep.tile([P, 2, T], F32, name=f"pair{u}") for u in range(2)]
         singles = [keep.tile([P, T], F32, name=f"single{j}", tag=f"single{j}", align_bytes=64) for j in range(PACK)]
-        w_codes = [keep.tile([P, PASSES, P], U32, name=f"w_codes{b}", align_bytes=64) for b in range(BLOCKS)]
+        w_codes = keep.tile([P, PASSES, N], U32, name="w_codes", align_bytes=64)
         w_scale = keep.tile([P, N], U8, name="w_scale", align_bytes=64)
         gam = [keep.tile([P, U], F32, name=f"gam{b}") for b in range(BLOCKS)]
         bet = [keep.tile([P, U], F32, name=f"bet{b}") for b in range(BLOCKS)]
@@ -59,21 +60,20 @@ def tile_picked_cbn_silu_e_kernel(tc, xT, w1_words, w1_scales, gamma, beta, offs
         for j in range(LAST):
             nc.sync.dma_start(singles[j][:], x_rows[1, :, j, :])
         nc.sync.dma_start(cls_sb[:], cls)
-        for lo, hi in ((0, CUT), (CUT, T)):
+        for lo, hi in CHUNKS:
             nc.sync.dma_start(singles[LAST][:, lo:hi], x_rows[1, :, LAST, lo:hi])
-        nc.sync.dma_start(bet[0][:], beta[0:P, :])
         scales_i32 = w1_scales.bitcast(I32)
         for q in range(4):
             nc.sync.dma_start(w_scale[:].bitcast(I32)[32 * q : 32 * q + 4 * PASSES, :], scales_i32[:, 4 * q : 4 * q + 4, :])
         w_rows = w1_words.rearrange("z p n r -> p z (n r)").bitcast(I32)
-        for b in range(BLOCKS):
-            nc.sync.dma_start(w_codes[b][:].bitcast(I32), w_rows[:, :, b * P : (b + 1) * P])
+        nc.sync.dma_start(w_codes[:].bitcast(I32), w_rows)
+        nc.sync.dma_start(bet[0][:], beta[0:P, :])
         for b in range(BLOCKS):
             nc.sync.dma_start(gam[b][:], gamma[b * P : (b + 1) * P, :])
         nc.sync.dma_start(bet[1][:], beta[P:N, :])
 
         picked0 = keep.tile([P, S, PACK], BF16, name="picked0", align_bytes=64)
-        picked1 = [keep.tile([P, HALF, PACK], BF16, name=f"picked1{h}", tag=f"half{h}", align_bytes=64) for h in range(2)]
+        picked1 = [keep.tile([P, HALF, PACK], BF16, name=f"picked1{h}", align_bytes=64) for h in range(2)]
         scale = [keep.tile([P, S], U8, name=f"scale{z}", align_bytes=64) for z in range(PASSES)]
 
         def by_offs(window, lo, hi):
@@ -107,17 +107,21 @@ def tile_picked_cbn_silu_e_kernel(tc, xT, w1_words, w1_scales, gamma, beta, offs
         nc.vector.tensor_copy(flat1[:, 2, HALF:S], by_offs(singles[2][:], HALF, S))
         nc.vector.tensor_copy(picked1[0][:, :, 2], by_offs(singles[2][:], 0, HALF))
         nc.scalar.copy(picked1[1][:, :, 0:LAST], flat1[:, :, HALF:S].rearrange("p j s -> p s j"))
-        nc.scalar.copy(rounded[:, 0:SCALAR_CAST], singles[LAST][:, 0:SCALAR_CAST])
-        nc.vector.tensor_copy(rounded[:, SCALAR_CAST:CUT], singles[LAST][:, SCALAR_CAST:CUT])
-        nc.scalar.copy(rounded[:, CUT:T], singles[LAST][:, CUT:T])
+        for engine_copy, lo, hi in (
+            (nc.scalar.copy, 0, SCALAR_HEAD),
+            (nc.vector.tensor_copy, SCALAR_HEAD, CHUNKS[0][1]),
+            (nc.vector.tensor_copy, CHUNKS[1][0], CHUNKS[1][1]),
+            (nc.vector.tensor_copy, CHUNKS[2][0], VECTOR_END),
+            (nc.scalar.copy, VECTOR_END, T),
+        ):
+            engine_copy(rounded[:, lo:hi], singles[LAST][:, lo:hi])
         nc.vector.tensor_copy(picked1[0][:, :, LAST], by_offs(singles[LAST][:], 0, HALF))
         nc.scalar.activation(picked1[1][:, :, LAST], by_offs(rounded[:], HALF, S), COPY)
         codes.append(keep.tile([P, S], U32, name="codes1", align_bytes=64))
-        shift0 = []
         for h, (lo, hi) in enumerate(HALVES):
             quantize(1, lo, hi, picked1[h][:])
-            shift0.append(keep.tile([P, HALF], F32, name=f"shift0{h}", tag=("shift00", "half1")[h], align_bytes=64))
-            nc.vector.tensor_copy(shift0[h][:], by_cls(bet[0][:], lo, hi))
+        shift0 = keep.tile([P, S], F32, name="shift0")
+        nc.vector.tensor_copy(shift0[:], by_cls(bet[0][:], 0, S))
 
         y = [keep.tile([P, S], F32, name=f"y{b}", tag=f"sums{b}") for b in range(BLOCKS)]
         acc = [[psum.tile([P, HALF], F32, name=f"acc{b}{h}", tag=f"bank{b}{h}") for h in range(2)] for b in range(BLOCKS)]
@@ -126,7 +130,7 @@ def tile_picked_cbn_silu_e_kernel(tc, xT, w1_words, w1_scales, gamma, beta, offs
                 for z in range(PASSES):
                     nc.tensor.matmul_mx(
                         out=acc[b][h][:],
-                        lhsT=w_codes[b][:, z, :].bitcast(FP8X4),
+                        lhsT=w_codes[:, z, b * P : (b + 1) * P].bitcast(FP8X4),
                         lhsT_scale=w_scale[4 * z :, b * P : (b + 1) * P],
                         rhs=codes[z][:, lo:hi].bitcast(FP8X4),
                         rhs_scale=scale[z][:, lo:hi],
@@ -144,7 +148,7 @@ def tile_picked_cbn_silu_e_kernel(tc, xT, w1_words, w1_scales, gamma, beta, offs
             sums = psum.tile([P, HALF], F32, name=f"sums{h}", tag=f"bank0{h}")
             back = psum.tile([P, HALF], F32, name=f"back{h}")
             for c in range(lo, hi, P):
-                nc.tensor.matmul(sums[:, c - lo : c - lo + P], shift0[h][:, c - lo : c - lo + P], ident[:], start=(c == lo), stop=False, is_transpose=True)
+                nc.tensor.matmul(sums[:, c - lo : c - lo + P], shift0[:, c : c + P], ident[:], start=(c == lo), stop=False, is_transpose=True)
             nc.vector.tensor_tensor(scaled[0][:, lo:hi], by_cls(gam[0][:], lo, hi), y[0][:, lo:hi], MULT)
             for c in range(lo, hi, P):
                 nc.tensor.matmul(sums[:, c - lo : c - lo + P], scaled[0][:, c : c + P], ident[:], start=False, stop=(c == hi - P), is_transpose=True)

@@ -1,7 +1,6 @@
 from contextlib import ExitStack
 
 import concourse.mybir as mybir
-from concourse.masks import make_identity
 
 K, T, S, N, U = 1024, 2048, 512, 256, 1024
 FLOPS = 2 * K * N * S
@@ -24,11 +23,7 @@ PASSES = K // (P * PACK)
 BLOCKS = N // P
 HALF = S // 2
 LAST = PACK - 1
-CHUNKS = ((0, 1152), (1152, 1664), (1664, T))
-SCALAR_HEAD = 512
-VECTOR_END = 1856
 HALVES = ((0, HALF), (HALF, S))
-ENDS = ((0, 256), (256, 384), (384, 512))
 
 
 def tile_picked_cbn_silu_e_kernel(tc, xT, w1_words, w1_scales, gamma, beta, offs, cls, out):
@@ -40,17 +35,17 @@ def tile_picked_cbn_silu_e_kernel(tc, xT, w1_words, w1_scales, gamma, beta, offs
         offs_sb = keep.tile([P, S // 16], U16, name="offs_sb")
         cls_sb = keep.tile([P, S // 16], U16, name="cls_sb")
         pairs = [keep.tile([P, 2, T], F32, name=f"pair{u}") for u in range(2)]
-        singles = [keep.tile([P, T], F32, name=f"single{j}", tag=f"single{j}", align_bytes=64) for j in range(PACK)]
+        singles = [keep.tile([P, T], F32, name=f"single{j}") for j in range(PACK)]
         w_codes = keep.tile([P, PASSES, N], U32, name="w_codes", align_bytes=64)
         w_scale = keep.tile([P, N], U8, name="w_scale", align_bytes=64)
         gam = [keep.tile([P, U], F32, name=f"gam{b}") for b in range(BLOCKS)]
         bet = [keep.tile([P, U], F32, name=f"bet{b}") for b in range(BLOCKS)]
 
         nc.vector.memset(w_scale[:].bitcast(I32), 0)
-        ident = keep.tile([P, P], F32, name="ident")
-        make_identity(nc, ident[:])
+        warm_in = keep.tile([P, 1], F32, name="warm_in")
         warm = keep.tile([P, 1], F32, name="warm")
-        nc.scalar.activation(warm[:], ident[:, 0:1], SILU)
+        nc.vector.memset(warm_in[:], 0.0)
+        nc.scalar.activation(warm[:], warm_in[:], SILU)
 
         x_rows = xT.rearrange("(z p j) t -> z p j t", z=PASSES, j=PACK)
         for u in range(2):
@@ -60,20 +55,18 @@ def tile_picked_cbn_silu_e_kernel(tc, xT, w1_words, w1_scales, gamma, beta, offs
         for j in range(LAST):
             nc.sync.dma_start(singles[j][:], x_rows[1, :, j, :])
         nc.sync.dma_start(cls_sb[:], cls)
-        for lo, hi in CHUNKS:
-            nc.sync.dma_start(singles[LAST][:, lo:hi], x_rows[1, :, LAST, lo:hi])
+        nc.sync.dma_start(singles[LAST][:], x_rows[1, :, LAST, :])
         scales_i32 = w1_scales.bitcast(I32)
         for q in range(4):
             nc.sync.dma_start(w_scale[:].bitcast(I32)[32 * q : 32 * q + 4 * PASSES, :], scales_i32[:, 4 * q : 4 * q + 4, :])
         w_rows = w1_words.rearrange("z p n r -> p z (n r)").bitcast(I32)
         nc.sync.dma_start(w_codes[:].bitcast(I32), w_rows)
-        nc.sync.dma_start(bet[0][:], beta[0:P, :])
-        for b in range(BLOCKS):
-            nc.sync.dma_start(gam[b][:], gamma[b * P : (b + 1) * P, :])
-        nc.sync.dma_start(bet[1][:], beta[P:N, :])
+        for tiles, table in ((gam, gamma), (bet, beta)):
+            for b in range(BLOCKS):
+                nc.sync.dma_start(tiles[b][:], table[b * P : (b + 1) * P, :])
 
-        picked0 = keep.tile([P, S, PACK], BF16, name="picked0", align_bytes=64)
-        picked1 = [keep.tile([P, HALF, PACK], BF16, name=f"picked1{h}", align_bytes=64) for h in range(2)]
+        picked = [[keep.tile([P, HALF, PACK], BF16, name=f"picked{z}{h}", align_bytes=64) for h in range(2)] for z in range(PASSES)]
+        codes = [keep.tile([P, S], U32, name=f"codes{z}", align_bytes=64) for z in range(PASSES)]
         scale = [keep.tile([P, S], U8, name=f"scale{z}", align_bytes=64) for z in range(PASSES)]
 
         def by_offs(window, lo, hi):
@@ -82,52 +75,39 @@ def tile_picked_cbn_silu_e_kernel(tc, xT, w1_words, w1_scales, gamma, beta, offs
         def by_cls(window, lo, hi):
             return window.indirect(cls_sb[:, lo // 16 : hi // 16])
 
-        def quantize(z, lo, hi, values):
+        def quantize(z, h):
+            lo, hi = HALVES[h]
             nc.vector.quantize_mx(
                 out=codes[z][:, lo:hi].bitcast(FP8X4),
                 scales=scale[z][:, lo:hi],
-                in_=values.rearrange("p s j -> p (s j)"),
+                in_=picked[z][h][:].rearrange("p s j -> p (s j)"),
             )
 
-        for j in range(2):
-            nc.vector.tensor_copy(picked0[:, :, j], by_offs(pairs[0][:, j, :], 0, S))
-        for h, (lo, hi) in enumerate(HALVES):
-            flat0 = keep.tile([P, 2, HALF], F32, name=f"flat0{h}")
-            for j in range(2):
-                nc.vector.tensor_copy(flat0[:, j, :], by_offs(pairs[1][:, j, :], lo, hi))
-            nc.scalar.copy(picked0[:, lo:hi, 2:4], flat0[:].rearrange("p j s -> p s j"))
+        flat0 = keep.tile([P, PACK, HALF], F32, name="flat0")
+        for j in range(PACK):
+            plane = pairs[j // 2][:, j % 2, :]
+            nc.vector.tensor_copy(picked[0][0][:, :, j], by_offs(plane, 0, HALF))
+            nc.scalar.activation(flat0[:, j, :], by_offs(plane, HALF, S), COPY)
+        nc.scalar.copy(picked[0][1][:], flat0[:].rearrange("p j s -> p s j"))
+        for h in range(2):
+            quantize(0, h)
 
-        flat1 = keep.tile([P, LAST, S], F32, name="flat1")
-        rounded = keep.tile([P, T], BF16, name="rounded", tag="sums0")
-        nc.vector.tensor_copy(flat1[:, 0, :], by_offs(singles[0][:], 0, S))
-        codes = [keep.tile([P, S], U32, name="codes0", tag="single0", align_bytes=64)]
-        quantize(0, 0, S, picked0[:])
-        nc.vector.tensor_copy(flat1[:, 1, :], by_offs(singles[1][:], 0, S))
-        nc.scalar.copy(picked1[0][:, :, 0:2], flat1[:, 0:2, 0:HALF].rearrange("p j s -> p s j"))
-        nc.vector.tensor_copy(flat1[:, 2, HALF:S], by_offs(singles[2][:], HALF, S))
-        nc.vector.tensor_copy(picked1[0][:, :, 2], by_offs(singles[2][:], 0, HALF))
-        nc.scalar.copy(picked1[1][:, :, 0:LAST], flat1[:, :, HALF:S].rearrange("p j s -> p s j"))
-        for engine_copy, lo, hi in (
-            (nc.scalar.copy, 0, SCALAR_HEAD),
-            (nc.vector.tensor_copy, SCALAR_HEAD, CHUNKS[0][1]),
-            (nc.vector.tensor_copy, CHUNKS[1][0], CHUNKS[1][1]),
-            (nc.vector.tensor_copy, CHUNKS[2][0], VECTOR_END),
-            (nc.scalar.copy, VECTOR_END, T),
-        ):
-            engine_copy(rounded[:, lo:hi], singles[LAST][:, lo:hi])
-        nc.vector.tensor_copy(picked1[0][:, :, LAST], by_offs(singles[LAST][:], 0, HALF))
-        nc.scalar.activation(picked1[1][:, :, LAST], by_offs(rounded[:], HALF, S), COPY)
-        codes.append(keep.tile([P, S], U32, name="codes1", align_bytes=64))
-        for h, (lo, hi) in enumerate(HALVES):
-            quantize(1, lo, hi, picked1[h][:])
-        shift0 = keep.tile([P, S], F32, name="shift0")
-        nc.vector.tensor_copy(shift0[:], by_cls(bet[0][:], 0, S))
+        flat1 = keep.tile([P, LAST, HALF], F32, name="flat1")
+        flat_last = keep.tile([P, HALF], F32, name="flat_last")
+        for j in range(LAST):
+            nc.vector.tensor_copy(picked[1][0][:, :, j], by_offs(singles[j][:], 0, HALF))
+            nc.scalar.activation(flat1[:, j, :], by_offs(singles[j][:], HALF, S), COPY)
+        nc.scalar.copy(picked[1][1][:, :, 0:LAST], flat1[:].rearrange("p j s -> p s j"))
+        nc.vector.tensor_copy(picked[1][0][:, :, LAST], by_offs(singles[LAST][:], 0, HALF))
+        nc.scalar.activation(flat_last[:], by_offs(singles[LAST][:], HALF, S), COPY)
+        nc.scalar.copy(picked[1][1][:, :, LAST], flat_last[:])
+        for h in range(2):
+            quantize(1, h)
 
-        y = [keep.tile([P, S], F32, name=f"y{b}", tag=f"sums{b}") for b in range(BLOCKS)]
-        acc = [[psum.tile([P, HALF], F32, name=f"acc{b}{h}", tag=f"bank{b}{h}") for h in range(2)] for b in range(BLOCKS)]
-        for b in range(BLOCKS):
-            for h, (lo, hi) in enumerate(HALVES):
-                for z in range(PASSES):
+        acc = [[psum.tile([P, HALF], F32, name=f"acc{b}{h}") for h in range(2)] for b in range(BLOCKS)]
+        for z in range(PASSES):
+            for b in range(BLOCKS):
+                for h, (lo, hi) in enumerate(HALVES):
                     nc.tensor.matmul_mx(
                         out=acc[b][h][:],
                         lhsT=w_codes[:, z, b * P : (b + 1) * P].bitcast(FP8X4),
@@ -137,31 +117,22 @@ def tile_picked_cbn_silu_e_kernel(tc, xT, w1_words, w1_scales, gamma, beta, offs
                         start=(z == 0),
                         stop=(z == PASSES - 1),
                     )
+
+        gain = [[keep.tile([P, HALF], F32, name=f"gain{b}{h}") for h in range(2)] for b in range(BLOCKS)]
+        scaled = [[keep.tile([P, HALF], F32, name=f"scaled{b}{h}") for h in range(2)] for b in range(BLOCKS)]
         for b in range(BLOCKS):
             for h, (lo, hi) in enumerate(HALVES):
-                nc.scalar.copy(y[b][:, lo:hi], acc[b][h][:])
+                nc.scalar.activation(gain[b][h][:], by_cls(gam[b][:], lo, hi), COPY)
+                nc.vector.tensor_tensor(scaled[b][h][:], acc[b][h][:], gain[b][h][:], MULT)
 
-        scaled = [keep.tile([P, S], F32, name=f"scaled{b}") for b in range(BLOCKS)]
-        res = [keep.tile([P, S], F32, name=f"res{b}") for b in range(BLOCKS)]
-        turned = keep.tile([P, S], F32, name="turned")
-        for h, (lo, hi) in enumerate(HALVES):
-            sums = psum.tile([P, HALF], F32, name=f"sums{h}", tag=f"bank0{h}")
-            back = psum.tile([P, HALF], F32, name=f"back{h}")
-            for c in range(lo, hi, P):
-                nc.tensor.matmul(sums[:, c - lo : c - lo + P], shift0[:, c : c + P], ident[:], start=(c == lo), stop=False, is_transpose=True)
-            nc.vector.tensor_tensor(scaled[0][:, lo:hi], by_cls(gam[0][:], lo, hi), y[0][:, lo:hi], MULT)
-            for c in range(lo, hi, P):
-                nc.tensor.matmul(sums[:, c - lo : c - lo + P], scaled[0][:, c : c + P], ident[:], start=False, stop=(c == hi - P), is_transpose=True)
-            nc.scalar.activation(turned[:, lo:hi], sums[:], SILU)
-            for c in range(lo, hi, P):
-                nc.tensor.transpose(back[:, c - lo : c - lo + P], turned[:, c : c + P], ident[:])
-            nc.scalar.copy(res[0][:, lo:hi], back[:])
-            nc.sync.dma_start(out[0:P, lo:hi], res[0][:, lo:hi])
-
-        shifted = keep.tile([P, S], F32, name="shifted")
-        for lo, hi in HALVES:
-            nc.vector.tensor_tensor(scaled[1][:, lo:hi], by_cls(gam[1][:], lo, hi), y[1][:, lo:hi], MULT)
-        for lo, hi in ENDS:
-            nc.vector.tensor_tensor(shifted[:, lo:hi], by_cls(bet[1][:], lo, hi), scaled[1][:, lo:hi], ADD)
-            nc.scalar.activation(res[1][:, lo:hi], shifted[:, lo:hi], SILU)
-            nc.sync.dma_start(out[P:N, lo:hi], res[1][:, lo:hi])
+        for b in range(BLOCKS):
+            rows = slice(b * P, (b + 1) * P)
+            shift = keep.tile([P, HALF], F32, name=f"shift{b}")
+            shifted = [keep.tile([P, HALF], F32, name=f"shifted{b}{h}") for h in range(2)]
+            res = [keep.tile([P, HALF], F32, name=f"res{b}{h}") for h in range(2)]
+            nc.scalar.activation(shift[:], by_cls(bet[b][:], HALF, S), COPY)
+            nc.vector.tensor_tensor(shifted[0][:], by_cls(bet[b][:], 0, HALF), scaled[b][0][:], ADD)
+            nc.vector.tensor_tensor(shifted[1][:], shift[:], scaled[b][1][:], ADD)
+            for h, (lo, hi) in enumerate(HALVES):
+                nc.scalar.activation(res[h][:], shifted[h][:], SILU)
+                nc.sync.dma_start(out[rows, lo:hi], res[h][:])

@@ -24,6 +24,8 @@ BLOCKS = N // P
 HALF = S // 2
 LAST = PACK - 1
 HALVES = ((0, HALF), (HALF, S))
+GAIN_SPLIT = 384
+ENDS = ((0, 256), (256, 384), (384, 512))
 
 
 def tile_picked_cbn_silu_e_kernel(tc, xT, w1_words, w1_scales, gamma, beta, offs, cls, out):
@@ -92,15 +94,17 @@ def tile_picked_cbn_silu_e_kernel(tc, xT, w1_words, w1_scales, gamma, beta, offs
         for h in range(2):
             quantize(0, h)
 
-        flat1 = keep.tile([P, LAST, HALF], F32, name="flat1")
-        flat_last = keep.tile([P, HALF], F32, name="flat_last")
+        flat1 = [keep.tile([P, 2, HALF], F32, name=f"flat1{u}") for u in range(2)]
         for j in range(LAST):
             nc.vector.tensor_copy(picked[1][0][:, :, j], by_offs(singles[j][:], 0, HALF))
-            nc.scalar.activation(flat1[:, j, :], by_offs(singles[j][:], HALF, S), COPY)
-        nc.scalar.copy(picked[1][1][:, :, 0:LAST], flat1[:].rearrange("p j s -> p s j"))
+            nc.scalar.activation(flat1[j // 2][:, j % 2, :], by_offs(singles[j][:], HALF, S), COPY)
+            if j == 1:
+                nc.scalar.copy(picked[1][1][:, :, 0:2], flat1[0][:].rearrange("p j s -> p s j"))
         nc.vector.tensor_copy(picked[1][0][:, :, LAST], by_offs(singles[LAST][:], 0, HALF))
-        nc.scalar.activation(flat_last[:], by_offs(singles[LAST][:], HALF, S), COPY)
-        nc.scalar.copy(picked[1][1][:, :, LAST], flat_last[:])
+        for engine_copy, lo, hi in ((nc.vector.tensor_copy, 0, P), (nc.scalar.copy, P, HALF)):
+            nc.scalar.activation(flat1[1][:, 1, lo:hi], by_offs(singles[LAST][:], HALF + lo, HALF + hi), COPY)
+        for engine_copy, lo, hi in ((nc.vector.tensor_copy, 0, P), (nc.scalar.copy, P, HALF)):
+            engine_copy(picked[1][1][:, lo:hi, 2:4], flat1[1][:, :, lo:hi].rearrange("p j s -> p s j"))
         for h in range(2):
             quantize(1, h)
 
@@ -118,21 +122,28 @@ def tile_picked_cbn_silu_e_kernel(tc, xT, w1_words, w1_scales, gamma, beta, offs
                         stop=(z == PASSES - 1),
                     )
 
-        gain = [[keep.tile([P, HALF], F32, name=f"gain{b}{h}") for h in range(2)] for b in range(BLOCKS)]
-        scaled = [[keep.tile([P, HALF], F32, name=f"scaled{b}{h}") for h in range(2)] for b in range(BLOCKS)]
+        scaled = [keep.tile([P, S], F32, name=f"scaled{b}") for b in range(BLOCKS)]
         for b in range(BLOCKS):
+            gain = keep.tile([P, S], F32, name=f"gain{b}")
+            nc.scalar.activation(gain[:, 0:HALF], by_cls(gam[b][:], 0, HALF), COPY)
+            nc.scalar.activation(gain[:, HALF:GAIN_SPLIT], by_cls(gam[b][:], HALF, GAIN_SPLIT), COPY)
+            nc.vector.tensor_copy(gain[:, GAIN_SPLIT:S], by_cls(gam[b][:], GAIN_SPLIT, S))
             for h, (lo, hi) in enumerate(HALVES):
-                nc.scalar.activation(gain[b][h][:], by_cls(gam[b][:], lo, hi), COPY)
-                nc.vector.tensor_tensor(scaled[b][h][:], acc[b][h][:], gain[b][h][:], MULT)
+                nc.vector.tensor_tensor(scaled[b][:, lo:hi], acc[b][h][:], gain[:, lo:hi], MULT)
 
-        for b in range(BLOCKS):
-            rows = slice(b * P, (b + 1) * P)
-            shift = keep.tile([P, HALF], F32, name=f"shift{b}")
-            shifted = [keep.tile([P, HALF], F32, name=f"shifted{b}{h}") for h in range(2)]
-            res = [keep.tile([P, HALF], F32, name=f"res{b}{h}") for h in range(2)]
-            nc.scalar.activation(shift[:], by_cls(bet[b][:], HALF, S), COPY)
-            nc.vector.tensor_tensor(shifted[0][:], by_cls(bet[b][:], 0, HALF), scaled[b][0][:], ADD)
-            nc.vector.tensor_tensor(shifted[1][:], shift[:], scaled[b][1][:], ADD)
-            for h, (lo, hi) in enumerate(HALVES):
-                nc.scalar.activation(res[h][:], shifted[h][:], SILU)
-                nc.sync.dma_start(out[rows, lo:hi], res[h][:])
+        shifted = [keep.tile([P, S], F32, name=f"shifted{b}") for b in range(BLOCKS)]
+        res = [keep.tile([P, S], F32, name=f"res{b}") for b in range(BLOCKS)]
+
+        def finish(b, lo, hi):
+            nc.scalar.activation(res[b][:, lo:hi], shifted[b][:, lo:hi], SILU)
+            nc.sync.dma_start(out[b * P : (b + 1) * P, lo:hi], res[b][:, lo:hi])
+
+        shift = keep.tile([P, HALF], F32, name="shift")
+        nc.scalar.activation(shift[:], by_cls(bet[0][:], HALF, S), COPY)
+        nc.vector.tensor_tensor(shifted[0][:, 0:HALF], by_cls(bet[0][:], 0, HALF), scaled[0][:, 0:HALF], ADD)
+        nc.vector.tensor_tensor(shifted[0][:, HALF:S], shift[:], scaled[0][:, HALF:S], ADD)
+        for lo, hi in HALVES:
+            finish(0, lo, hi)
+        for lo, hi in ENDS:
+            nc.vector.tensor_tensor(shifted[1][:, lo:hi], by_cls(bet[1][:], lo, hi), scaled[1][:, lo:hi], ADD)
+            finish(1, lo, hi)

@@ -25,7 +25,6 @@ HALF = S // 2
 LAST = PACK - 1
 HALVES = ((0, HALF), (HALF, S))
 GAIN_SPLIT = 384
-ENDS = ((0, 256), (256, 384), (384, 512))
 
 
 def tile_picked_cbn_silu_e_kernel(tc, xT, w1_words, w1_scales, gamma, beta, offs, cls, out):
@@ -138,12 +137,26 @@ def tile_picked_cbn_silu_e_kernel(tc, xT, w1_words, w1_scales, gamma, beta, offs
             nc.scalar.activation(res[b][:, lo:hi], shifted[b][:, lo:hi], SILU)
             nc.sync.dma_start(out[b * P : (b + 1) * P, lo:hi], res[b][:, lo:hi])
 
-        shift = keep.tile([P, HALF], F32, name="shift")
-        nc.scalar.activation(shift[:], by_cls(bet[0][:], HALF, S), COPY)
-        nc.vector.tensor_tensor(shifted[0][:, 0:HALF], by_cls(bet[0][:], 0, HALF), scaled[0][:, 0:HALF], ADD)
-        nc.vector.tensor_tensor(shifted[0][:, HALF:S], shift[:], scaled[0][:, HALF:S], ADD)
-        for lo, hi in HALVES:
+        shift = [keep.tile([P, S], F32, name=f"shift{b}") for b in range(BLOCKS)]
+
+        def fused_add(b, lo, hi):
+            nc.vector.tensor_tensor(shifted[b][:, lo:hi], by_cls(bet[b][:], lo, hi), scaled[b][:, lo:hi], ADD)
+
+        def look_up(b, lo, hi):
+            nc.scalar.activation(shift[b][:, lo:hi], by_cls(bet[b][:], lo, hi), COPY)
+
+        def plain_add(b, lo, hi):
+            nc.vector.tensor_tensor(shifted[b][:, lo:hi], shift[b][:, lo:hi], scaled[b][:, lo:hi], ADD)
+
+        fused_add(0, 0, 192)
+        finish(0, 0, 192)
+        for lo, hi in ((192, 384), (384, S)):
+            look_up(0, lo, hi)
+            plain_add(0, lo, hi)
             finish(0, lo, hi)
-        for lo, hi in ENDS:
-            nc.vector.tensor_tensor(shifted[1][:, lo:hi], by_cls(bet[1][:], lo, hi), scaled[1][:, lo:hi], ADD)
+        look_up(1, 384, S)
+        for lo, hi in ((0, 128), (128, 256), (256, 384)):
+            fused_add(1, lo, hi)
             finish(1, lo, hi)
+        plain_add(1, 384, S)
+        finish(1, 384, S)

@@ -59,7 +59,7 @@ def tile_picked_cbn_silu_e_kernel(tc, xT, w1_words, w1_scales, gamma, beta, offs
         nc.sync.dma_start(singles[LAST][:], x_rows[1, :, LAST, :])
         scales_i32 = w1_scales.bitcast(I32)
         for q in range(4):
-            nc.sync.dma_start(w_scale[:].bitcast(I32)[32 * q : 32 * q + 4 * PASSES, :], scales_i32[:, 4 * q : 4 * q + 4, :])
+            nc.scalar.dma_start(w_scale[:].bitcast(I32)[32 * q : 32 * q + 4 * PASSES, :], scales_i32[:, 4 * q : 4 * q + 4, :])
         w_rows = w1_words.rearrange("z p n r -> p z (n r)").bitcast(I32)
         nc.sync.dma_start(w_codes[:].bitcast(I32), w_rows)
         for tiles, table in ((gam, gamma), (bet, beta)):

@@ -35,9 +35,11 @@ def tile_picked_cbn_silu_e_kernel(tc, xT, w1_words, w1_scales, gamma, beta, offs
 
         offs_sb = keep.tile([P, S // 16], U16, name="offs_sb")
         cls_sb = keep.tile([P, S // 16], U16, name="cls_sb")
-        pairs = [keep.tile([P, 2, T], F32, name=f"pair{u}") for u in range(2)]
-        singles = [keep.tile([P, T], F32, name=f"single{j}") for j in range(PACK)]
-        w_codes = keep.tile([P, PASSES, N], U32, name="w_codes", align_bytes=64)
+        x_first = keep.tile([P, PACK, T], F32, name="x_first")
+        x_pair = keep.tile([P, 2, T], F32, name="x_pair")
+        singles = {j: keep.tile([P, T], F32, name=f"single{j}", tag=f"single{j}", align_bytes=64) for j in (2, LAST)}
+        w_first = keep.tile([P, N], U32, name="w_first", align_bytes=64)
+        w_second = [keep.tile([P, P], U32, name=f"w_second{b}", align_bytes=64) for b in range(BLOCKS)]
         w_scale = keep.tile([P, N], U8, name="w_scale", align_bytes=64)
         gam = [keep.tile([P, U], F32, name=f"gam{b}") for b in range(BLOCKS)]
         bet = [keep.tile([P, U], F32, name=f"bet{b}") for b in range(BLOCKS)]
@@ -49,25 +51,26 @@ def tile_picked_cbn_silu_e_kernel(tc, xT, w1_words, w1_scales, gamma, beta, offs
         nc.scalar.activation(warm[:], warm_in[:], SILU)
 
         x_rows = xT.rearrange("(z p j) t -> z p j t", z=PASSES, j=PACK)
-        for u in range(2):
-            nc.sync.dma_start(pairs[u][:], x_rows[0, :, 2 * u : 2 * u + 2, :])
-            if u == 0:
-                nc.sync.dma_start(offs_sb[:], offs)
-        for j in range(LAST):
-            nc.sync.dma_start(singles[j][:], x_rows[1, :, j, :])
-        nc.sync.dma_start(cls_sb[:], cls)
-        nc.sync.dma_start(singles[LAST][:], x_rows[1, :, LAST, :])
+        nc.sync.dma_start(x_first[:], x_rows[0])
         scales_i32 = w1_scales.bitcast(I32)
         for q in range(4):
-            nc.scalar.dma_start(w_scale[:].bitcast(I32)[32 * q : 32 * q + 4 * PASSES, :], scales_i32[:, 4 * q : 4 * q + 4, :])
+            nc.sync.dma_start(w_scale[:].bitcast(I32)[32 * q : 32 * q + 4 * PASSES, :], scales_i32[:, 4 * q : 4 * q + 4, :])
+        nc.sync.dma_start(offs_sb[:], offs)
+        nc.sync.dma_start(x_pair[:], x_rows[1, :, 0:2, :])
+        nc.sync.dma_start(singles[2][:], x_rows[1, :, 2, :])
+        nc.sync.dma_start(cls_sb[:], cls)
+        nc.sync.dma_start(singles[LAST][:], x_rows[1, :, LAST, :])
         w_rows = w1_words.rearrange("z p n r -> p z (n r)").bitcast(I32)
-        nc.sync.dma_start(w_codes[:].bitcast(I32), w_rows)
-        for tiles, table in ((gam, gamma), (bet, beta)):
-            for b in range(BLOCKS):
-                nc.sync.dma_start(tiles[b][:], table[b * P : (b + 1) * P, :])
+        nc.sync.dma_start(w_first[:].bitcast(I32), w_rows[:, 0, :])
+        nc.sync.dma_start(w_second[0][:].bitcast(I32), w_rows[:, 1, 0:P])
+        for b in range(BLOCKS):
+            nc.sync.dma_start(gam[b][:], gamma[b * P : (b + 1) * P, :])
+        nc.sync.dma_start(w_second[1][:].bitcast(I32), w_rows[:, 1, P:N])
+        for b in range(BLOCKS):
+            nc.sync.dma_start(bet[b][:], beta[b * P : (b + 1) * P, :])
 
         picked = [[keep.tile([P, HALF, PACK], BF16, name=f"picked{z}{h}", align_bytes=64) for h in range(2)] for z in range(PASSES)]
-        codes = [keep.tile([P, S], U32, name=f"codes{z}", align_bytes=64) for z in range(PASSES)]
+        codes = [keep.tile([P, S], U32, name="codes0", align_bytes=64)]
         scale = [keep.tile([P, S], U8, name=f"scale{z}", align_bytes=64) for z in range(PASSES)]
 
         def by_offs(window, lo, hi):
@@ -86,7 +89,7 @@ def tile_picked_cbn_silu_e_kernel(tc, xT, w1_words, w1_scales, gamma, beta, offs
 
         flat0 = keep.tile([P, PACK, HALF], F32, name="flat0")
         for j in range(PACK):
-            plane = pairs[j // 2][:, j % 2, :]
+            plane = x_first[:, j, :]
             nc.vector.tensor_copy(picked[0][0][:, :, j], by_offs(plane, 0, HALF))
             nc.scalar.activation(flat0[:, j, :], by_offs(plane, HALF, S), COPY)
         nc.scalar.copy(picked[0][1][:], flat0[:].rearrange("p j s -> p s j"))
@@ -95,8 +98,9 @@ def tile_picked_cbn_silu_e_kernel(tc, xT, w1_words, w1_scales, gamma, beta, offs
 
         flat1 = [keep.tile([P, 2, HALF], F32, name=f"flat1{u}") for u in range(2)]
         for j in range(LAST):
-            nc.vector.tensor_copy(picked[1][0][:, :, j], by_offs(singles[j][:], 0, HALF))
-            nc.scalar.activation(flat1[j // 2][:, j % 2, :], by_offs(singles[j][:], HALF, S), COPY)
+            plane = x_pair[:, j, :] if j < 2 else singles[j][:]
+            nc.vector.tensor_copy(picked[1][0][:, :, j], by_offs(plane, 0, HALF))
+            nc.scalar.activation(flat1[j // 2][:, j % 2, :], by_offs(plane, HALF, S), COPY)
             if j == 1:
                 nc.scalar.copy(picked[1][1][:, :, 0:2], flat1[0][:].rearrange("p j s -> p s j"))
         nc.vector.tensor_copy(picked[1][0][:, :, LAST], by_offs(singles[LAST][:], 0, HALF))
@@ -104,6 +108,7 @@ def tile_picked_cbn_silu_e_kernel(tc, xT, w1_words, w1_scales, gamma, beta, offs
             nc.scalar.activation(flat1[1][:, 1, lo:hi], by_offs(singles[LAST][:], HALF + lo, HALF + hi), COPY)
         for engine_copy, lo, hi in ((nc.vector.tensor_copy, 0, P), (nc.scalar.copy, P, HALF)):
             engine_copy(picked[1][1][:, lo:hi, 2:4], flat1[1][:, :, lo:hi].rearrange("p j s -> p s j"))
+        codes.append(keep.tile([P, S], U32, name="codes1", tag=f"single{LAST}", align_bytes=64))
         for h in range(2):
             quantize(1, h)
 
@@ -113,7 +118,7 @@ def tile_picked_cbn_silu_e_kernel(tc, xT, w1_words, w1_scales, gamma, beta, offs
                 for h, (lo, hi) in enumerate(HALVES):
                     nc.tensor.matmul_mx(
                         out=acc[b][h][:],
-                        lhsT=w_codes[:, z, b * P : (b + 1) * P].bitcast(FP8X4),
+                        lhsT=(w_second[b][:] if z else w_first[:, b * P : (b + 1) * P]).bitcast(FP8X4),
                         lhsT_scale=w_scale[4 * z :, b * P : (b + 1) * P],
                         rhs=codes[z][:, lo:hi].bitcast(FP8X4),
                         rhs_scale=scale[z][:, lo:hi],

@@ -35,14 +35,14 @@ def tile_picked_cbn_silu_e_kernel(tc, xT, w1_words, w1_scales, gamma, beta, offs
 
         offs_sb = keep.tile([P, S // 16], U16, name="offs_sb")
         cls_sb = keep.tile([P, S // 16], U16, name="cls_sb")
-        x_first = keep.tile([P, PACK, T], F32, name="x_first")
-        x_pair = keep.tile([P, 2, T], F32, name="x_pair")
-        singles = {j: keep.tile([P, T], F32, name=f"single{j}", tag=f"single{j}", align_bytes=64) for j in (2, LAST)}
-        w_first = keep.tile([P, N], U32, name="w_first", align_bytes=64)
-        w_second = [keep.tile([P, P], U32, name=f"w_second{b}", align_bytes=64) for b in range(BLOCKS)]
-        w_scale = keep.tile([P, N], U8, name="w_scale", align_bytes=64)
-        gam = [keep.tile([P, U], F32, name=f"gam{b}") for b in range(BLOCKS)]
-        bet = [keep.tile([P, U], F32, name=f"bet{b}") for b in range(BLOCKS)]
+        x_first = keep.tile([P, PACK, T], F32, name="x_first", align_bytes=256)
+        x_pair = keep.tile([P, 2, T], F32, name="x_pair", align_bytes=256)
+        singles = {j: keep.tile([P, T], F32, name=f"single{j}", tag=f"single{j}", align_bytes=256) for j in (2, LAST)}
+        w_first = keep.tile([P, N], U32, name="w_first", align_bytes=256)
+        w_second = [keep.tile([P, P], U32, name=f"w_second{b}", align_bytes=256) for b in range(BLOCKS)]
+        w_scale = keep.tile([P, N], U8, name="w_scale", align_bytes=256)
+        gam = [keep.tile([P, U], F32, name=f"gam{b}", align_bytes=256) for b in range(BLOCKS)]
+        bet = [keep.tile([P, U], F32, name=f"bet{b}", align_bytes=256) for b in range(BLOCKS)]
 
         nc.vector.memset(w_scale[:].bitcast(I32), 0)
         warm_in = keep.tile([P, 1], F32, name="warm_in")
@@ -96,19 +96,15 @@ def tile_picked_cbn_silu_e_kernel(tc, xT, w1_words, w1_scales, gamma, beta, offs
         for h in range(2):
             quantize(0, h)
 
-        flat1 = [keep.tile([P, 2, HALF], F32, name=f"flat1{u}") for u in range(2)]
-        for j in range(LAST):
-            plane = x_pair[:, j, :] if j < 2 else singles[j][:]
-            nc.vector.tensor_copy(picked[1][0][:, :, j], by_offs(plane, 0, HALF))
-            nc.scalar.activation(flat1[j // 2][:, j % 2, :], by_offs(plane, HALF, S), COPY)
-            if j == 1:
-                nc.scalar.copy(picked[1][1][:, :, 0:2], flat1[0][:].rearrange("p j s -> p s j"))
-        nc.vector.tensor_copy(picked[1][0][:, :, LAST], by_offs(singles[LAST][:], 0, HALF))
-        for engine_copy, lo, hi in ((nc.vector.tensor_copy, 0, P), (nc.scalar.copy, P, HALF)):
-            nc.scalar.activation(flat1[1][:, 1, lo:hi], by_offs(singles[LAST][:], HALF + lo, HALF + hi), COPY)
-        for engine_copy, lo, hi in ((nc.vector.tensor_copy, 0, P), (nc.scalar.copy, P, HALF)):
-            engine_copy(picked[1][1][:, lo:hi, 2:4], flat1[1][:, :, lo:hi].rearrange("p j s -> p s j"))
-        codes.append(keep.tile([P, S], U32, name="codes1", tag=f"single{LAST}", align_bytes=64))
+        flat1 = keep.tile([P, 2, HALF], F32, name="flat1")
+        for j in range(2):
+            nc.vector.tensor_copy(picked[1][0][:, :, j], by_offs(x_pair[:, j, :], 0, HALF))
+            nc.scalar.activation(flat1[:, j, :], by_offs(x_pair[:, j, :], HALF, S), COPY)
+        nc.scalar.copy(picked[1][1][:, :, 0:2], flat1[:].rearrange("p j s -> p s j"))
+        for j in (2, LAST):
+            nc.vector.tensor_copy(picked[1][0][:, :, j], by_offs(singles[j][:], 0, HALF))
+            nc.scalar.activation(picked[1][1][:, :, j], by_offs(singles[j][:], HALF, S), COPY)
+        codes.append(keep.tile([P, S], U32, name="codes1", align_bytes=64))
         for h in range(2):
             quantize(1, h)
 
@@ -136,7 +132,7 @@ def tile_picked_cbn_silu_e_kernel(tc, xT, w1_words, w1_scales, gamma, beta, offs
                 nc.vector.tensor_tensor(scaled[b][:, lo:hi], acc[b][h][:], gain[:, lo:hi], MULT)
 
         shifted = [keep.tile([P, S], F32, name=f"shifted{b}") for b in range(BLOCKS)]
-        res = [keep.tile([P, S], F32, name=f"res{b}") for b in range(BLOCKS)]
+        res = [keep.tile([P, S], F32, name=f"res{b}", align_bytes=256) for b in range(BLOCKS)]
 
         def finish(b, lo, hi):
             nc.scalar.activation(res[b][:, lo:hi], shifted[b][:, lo:hi], SILU)

@@ -38,8 +38,8 @@ def tile_picked_cbn_silu_e_kernel(tc, xT, w1_words, w1_scales, gamma, beta, offs
         x_first = keep.tile([P, PACK, T], F32, name="x_first", align_bytes=256)
         x_pair = keep.tile([P, 2, T], F32, name="x_pair", align_bytes=256)
         singles = {j: keep.tile([P, T], F32, name=f"single{j}", tag=f"single{j}", align_bytes=256) for j in (2, LAST)}
-        w_first = keep.tile([P, N], U32, name="w_first", align_bytes=256)
-        w_second = [keep.tile([P, P], U32, name=f"w_second{b}", align_bytes=256) for b in range(BLOCKS)]
+        w_band0 = keep.tile([P, PASSES, P], U32, name="w_band0", align_bytes=256)
+        w_band1 = [keep.tile([P, P], U32, name=f"w_band1{z}", align_bytes=256) for z in range(PASSES)]
         w_scale = keep.tile([P, N], U8, name="w_scale", align_bytes=256)
         gam = [keep.tile([P, U], F32, name=f"gam{b}", align_bytes=256) for b in range(BLOCKS)]
         bet = [keep.tile([P, U], F32, name=f"bet{b}", align_bytes=256) for b in range(BLOCKS)]
@@ -61,11 +61,10 @@ def tile_picked_cbn_silu_e_kernel(tc, xT, w1_words, w1_scales, gamma, beta, offs
         nc.sync.dma_start(cls_sb[:], cls)
         nc.sync.dma_start(singles[LAST][:], x_rows[1, :, LAST, :])
         w_rows = w1_words.rearrange("z p n r -> p z (n r)").bitcast(I32)
-        nc.sync.dma_start(w_first[:].bitcast(I32), w_rows[:, 0, :])
-        nc.sync.dma_start(w_second[0][:].bitcast(I32), w_rows[:, 1, 0:P])
+        nc.sync.dma_start(w_band0[:].bitcast(I32), w_rows[:, :, 0:P])
         for b in range(BLOCKS):
             nc.sync.dma_start(gam[b][:], gamma[b * P : (b + 1) * P, :])
-        nc.sync.dma_start(w_second[1][:].bitcast(I32), w_rows[:, 1, P:N])
+            nc.sync.dma_start(w_band1[b][:].bitcast(I32), w_rows[:, b, P:N])
         for b in range(BLOCKS):
             nc.sync.dma_start(bet[b][:], beta[b * P : (b + 1) * P, :])
 
@@ -109,12 +108,12 @@ def tile_picked_cbn_silu_e_kernel(tc, xT, w1_words, w1_scales, gamma, beta, offs
             quantize(1, h)
 
         acc = [[psum.tile([P, HALF], F32, name=f"acc{b}{h}") for h in range(2)] for b in range(BLOCKS)]
-        for z in range(PASSES):
-            for b in range(BLOCKS):
+        for b in range(BLOCKS):
+            for z in range(PASSES):
                 for h, (lo, hi) in enumerate(HALVES):
                     nc.tensor.matmul_mx(
                         out=acc[b][h][:],
-                        lhsT=(w_second[b][:] if z else w_first[:, b * P : (b + 1) * P]).bitcast(FP8X4),
+                        lhsT=(w_band1[z][:] if b else w_band0[:, z, :]).bitcast(FP8X4),
                         lhsT_scale=w_scale[4 * z :, b * P : (b + 1) * P],
                         rhs=codes[z][:, lo:hi].bitcast(FP8X4),
                         rhs_scale=scale[z][:, lo:hi],

from contextlib import ExitStack

import concourse.mybir as mybir

K, T, S, N, U = 1024, 2048, 512, 256, 1024
FLOPS = 2 * K * N * S

F32 = mybir.dt.float32
BF16 = mybir.dt.bfloat16
I32 = mybir.dt.int32
U32 = mybir.dt.uint32
U16 = mybir.dt.uint16
U8 = mybir.dt.uint8
FP8X4 = mybir.dt.float8_e4m3fn_x4
MULT = mybir.AluOpType.mult
ADD = mybir.AluOpType.add
SILU = mybir.ActivationFunctionType.Silu
COPY = mybir.ActivationFunctionType.Copy

P = 128
PACK = 4
PASSES = K // (P * PACK)
BLOCKS = N // P
HALF = S // 2
LAST = PACK - 1
HALVES = ((0, HALF), (HALF, S))
GAIN_SPLIT = 384


def tile_picked_cbn_silu_e_kernel(tc, xT, w1_words, w1_scales, gamma, beta, offs, cls, out):
    nc = tc.nc
    with ExitStack() as ctx:
        keep = ctx.enter_context(tc.tile_pool(name="keep", bufs=1))
        psum = ctx.enter_context(tc.psum_pool(name="psum", bufs=1))

        offs_sb = keep.tile([P, S // 16], U16, name="offs_sb")
        cls_sb = keep.tile([P, S // 16], U16, name="cls_sb")
        x_first = keep.tile([P, PACK, T], F32, name="x_first", align_bytes=256)
        x_pair = keep.tile([P, 2, T], F32, name="x_pair", align_bytes=256)
        singles = {j: keep.tile([P, T], F32, name=f"single{j}", tag=f"single{j}", align_bytes=256) for j in (2, LAST)}
        w_band0 = keep.tile([P, PASSES, P], U32, name="w_band0", align_bytes=256)
        w_band1 = [keep.tile([P, P], U32, name=f"w_band1{z}", align_bytes=256) for z in range(PASSES)]
        w_scale = keep.tile([P, N], U8, name="w_scale", align_bytes=256)
        gam = [keep.tile([P, U], F32, name=f"gam{b}", align_bytes=256) for b in range(BLOCKS)]
        bet = [keep.tile([P, U], F32, name=f"bet{b}", align_bytes=256) for b in range(BLOCKS)]

        nc.vector.memset(w_scale[:].bitcast(I32), 0)
        warm_in = keep.tile([P, 1], F32, name="warm_in")
        warm = keep.tile([P, 1], F32, name="warm")
        nc.vector.memset(warm_in[:], 0.0)
        nc.scalar.activation(warm[:], warm_in[:], SILU)

        x_rows = xT.rearrange("(z p j) t -> z p j t", z=PASSES, j=PACK)
        nc.sync.dma_start(x_first[:], x_rows[0])
        scales_i32 = w1_scales.bitcast(I32)
        for q in range(4):
            nc.sync.dma_start(w_scale[:].bitcast(I32)[32 * q : 32 * q + 4 * PASSES, :], scales_i32[:, 4 * q : 4 * q + 4, :])
        nc.sync.dma_start(offs_sb[:], offs)
        nc.sync.dma_start(x_pair[:], x_rows[1, :, 0:2, :])
        nc.sync.dma_start(singles[2][:], x_rows[1, :, 2, :])
        nc.sync.dma_start(cls_sb[:], cls)
        nc.sync.dma_start(singles[LAST][:], x_rows[1, :, LAST, :])
        w_rows = w1_words.rearrange("z p n r -> p z (n r)").bitcast(I32)
        nc.sync.dma_start(w_band0[:].bitcast(I32), w_rows[:, :, 0:P])
        for b in range(BLOCKS):
            nc.sync.dma_start(gam[b][:], gamma[b * P : (b + 1) * P, :])
            nc.sync.dma_start(w_band1[b][:].bitcast(I32), w_rows[:, b, P:N])
        for b in range(BLOCKS):
            nc.sync.dma_start(bet[b][:], beta[b * P : (b + 1) * P, :])

        picked = [[keep.tile([P, HALF, PACK], BF16, name=f"picked{z}{h}", align_bytes=64) for h in range(2)] for z in range(PASSES)]
        codes = [keep.tile([P, S], U32, name="codes0", align_bytes=64)]
        scale = [keep.tile([P, S], U8, name=f"scale{z}", align_bytes=64) for z in range(PASSES)]

        def by_offs(window, lo, hi):
            return window.indirect(offs_sb[:, lo // 16 : hi // 16])

        def by_cls(window, lo, hi):
            return window.indirect(cls_sb[:, lo // 16 : hi // 16])

        def quantize(z, h):
            lo, hi = HALVES[h]
            nc.vector.quantize_mx(
                out=codes[z][:, lo:hi].bitcast(FP8X4),
                scales=scale[z][:, lo:hi],
                in_=picked[z][h][:].rearrange("p s j -> p (s j)"),
            )

        flat0 = keep.tile([P, PACK, HALF], F32, name="flat0")
        for j in range(PACK):
            plane = x_first[:, j, :]
            nc.vector.tensor_copy(picked[0][0][:, :, j], by_offs(plane, 0, HALF))
            nc.scalar.activation(flat0[:, j, :], by_offs(plane, HALF, S), COPY)
        nc.scalar.copy(picked[0][1][:], flat0[:].rearrange("p j s -> p s j"))
        for h in range(2):
            quantize(0, h)

        flat1 = keep.tile([P, 2, HALF], F32, name="flat1")
        for j in range(2):
            nc.vector.tensor_copy(picked[1][0][:, :, j], by_offs(x_pair[:, j, :], 0, HALF))
            nc.scalar.activation(flat1[:, j, :], by_offs(x_pair[:, j, :], HALF, S), COPY)
        nc.scalar.copy(picked[1][1][:, :, 0:2], flat1[:].rearrange("p j s -> p s j"))
        for j in (2, LAST):
            nc.vector.tensor_copy(picked[1][0][:, :, j], by_offs(singles[j][:], 0, HALF))
            nc.scalar.activation(picked[1][1][:, :, j], by_offs(singles[j][:], HALF, S), COPY)
        codes.append(keep.tile([P, S], U32, name="codes1", align_bytes=64))
        for h in range(2):
            quantize(1, h)

        acc = [[psum.tile([P, HALF], F32, name=f"acc{b}{h}") for h in range(2)] for b in range(BLOCKS)]
        for b in range(BLOCKS):
            for z in range(PASSES):
                for h, (lo, hi) in enumerate(HALVES):
                    nc.tensor.matmul_mx(
                        out=acc[b][h][:],
                        lhsT=(w_band1[z][:] if b else w_band0[:, z, :]).bitcast(FP8X4),
                        lhsT_scale=w_scale[4 * z :, b * P : (b + 1) * P],
                        rhs=codes[z][:, lo:hi].bitcast(FP8X4),
                        rhs_scale=scale[z][:, lo:hi],
                        start=(z == 0),
                        stop=(z == PASSES - 1),
                    )

        scaled = [keep.tile([P, S], F32, name=f"scaled{b}") for b in range(BLOCKS)]
        for b in range(BLOCKS):
            gain = keep.tile([P, S], F32, name=f"gain{b}")
            nc.scalar.activation(gain[:, 0:HALF], by_cls(gam[b][:], 0, HALF), COPY)
            nc.scalar.activation(gain[:, HALF:GAIN_SPLIT], by_cls(gam[b][:], HALF, GAIN_SPLIT), COPY)
            nc.vector.tensor_copy(gain[:, GAIN_SPLIT:S], by_cls(gam[b][:], GAIN_SPLIT, S))
            for h, (lo, hi) in enumerate(HALVES):
                nc.vector.tensor_tensor(scaled[b][:, lo:hi], acc[b][h][:], gain[:, lo:hi], MULT)

        shifted = [keep.tile([P, S], F32, name=f"shifted{b}") for b in range(BLOCKS)]
        res = [keep.tile([P, S], F32, name=f"res{b}", align_bytes=256) for b in range(BLOCKS)]

        def finish(b, lo, hi):
            nc.scalar.activation(res[b][:, lo:hi], shifted[b][:, lo:hi], SILU)
            nc.sync.dma_start(out[b * P : (b + 1) * P, lo:hi], res[b][:, lo:hi])

        shift = [keep.tile([P, S], F32, name=f"shift{b}") for b in range(BLOCKS)]

        def fused_add(b, lo, hi):
            nc.vector.tensor_tensor(shifted[b][:, lo:hi], by_cls(bet[b][:], lo, hi), scaled[b][:, lo:hi], ADD)

        def look_up(b, lo, hi):
            nc.scalar.activation(shift[b][:, lo:hi], by_cls(bet[b][:], lo, hi), COPY)

        def plain_add(b, lo, hi):
            nc.vector.tensor_tensor(shifted[b][:, lo:hi], shift[b][:, lo:hi], scaled[b][:, lo:hi], ADD)

        fused_add(0, 0, 192)
        finish(0, 0, 192)
        for lo, hi in ((192, 384), (384, S)):
            look_up(0, lo, hi)
            plain_add(0, lo, hi)
            finish(0, lo, hi)
        look_up(1, 384, S)
        for lo, hi in ((0, 128), (128, 256), (256, 384)):
            fused_add(1, lo, hi)
            finish(1, lo, hi)
        plain_add(1, 384, S)
        finish(1, 384, S)
